import numpy as np
import ml_dtypes


def mxq(x, axis, fmt="e4m3"):
    dtype, down = {"e4m3": (ml_dtypes.float8_e4m3fn, 7), "e5m2": (ml_dtypes.float8_e5m2, 14)}[fmt]
    v = np.moveaxis(np.asarray(x, np.float32).astype(ml_dtypes.bfloat16).astype(np.float64), axis, -1)
    blocks = v.reshape(v.shape[:-1] + (-1, 32))
    amax = np.abs(blocks).max(-1, keepdims=True)
    byte = np.maximum(np.where(amax > 0, np.frexp(amax)[1] - 1 + 127, 0) - down, 1)
    scale = np.exp2(byte - 127.0)
    codes = (blocks / scale).astype(np.float32).astype(dtype).astype(np.float64)
    return np.moveaxis((codes * scale).reshape(v.shape), -1, axis)


WIDE = False


def mx_kscale(k):
    if not WIDE:
        return np.ones(k)
    levels = np.array([10, -10, 5, -5, 0])
    if k % 512:
        return np.exp2(np.random.permutation(np.resize(levels, k // 32))).repeat(32)
    a = np.empty((k // 512, 16))
    for p in range(k // 512):
        a[p, :8] = np.random.permutation(np.resize(levels, 8))
        for g in range(8):
            far = levels[np.abs(levels - a[p, g]) >= 10]
            a[p, g + 8] = far[np.random.randint(len(far))]
    return np.exp2(a.ravel()).repeat(32)


def f64(x):
    return np.asarray(x).astype(np.float64)


def striped(idx):
    return np.tile(idx.reshape(-1, 16).T, (8, 1)).astype(np.uint16)


def unstriped(offs):
    return offs[:16].T.reshape(-1).astype(np.int64)


E2M1 = np.array([0.0, 0.5, 1.0, 1.5, 2.0, 3.0, 4.0, 6.0, -0.0, -0.5, -1.0, -1.5, -2.0, -3.0, -4.0, -6.0])


def pack_weight(w, fmt):
    k, n = w.shape
    w = f64(np.asarray(w, np.float32).astype(ml_dtypes.bfloat16)).reshape(k // 32, 32, n)
    amax = np.abs(w).max(1)
    if fmt == "e4m3":
        byte = np.frexp(amax)[1] - 1 + 127 - 7
    else:
        mant, ex = np.frexp(amax / 6.0)
        byte = np.where(mant > 0.5, ex, ex - 1) + 127
    byte = np.clip(np.where(amax > 0, byte, 1), 1, 254)
    scaled = (w * np.exp2(127.0 - byte)[:, None, :]).reshape(k, n).astype(np.float32)
    by_word = np.ascontiguousarray(scaled.reshape(k // 512, 128, 4, n).transpose(0, 1, 3, 2))
    if fmt == "e4m3":
        words = by_word.astype(ml_dtypes.float8_e4m3fn).view(np.uint8)
    else:
        c = by_word.astype(ml_dtypes.float4_e2m1fn).view(np.uint8) & 0xF
        words = (c[..., 0::2] | (c[..., 1::2] << 4)).reshape(k // 512, 128, 2 * n)
    return np.ascontiguousarray(words), np.ascontiguousarray(byte.astype(np.uint8).reshape(k // 512, 16, n))


def unpack_weight(words, scales, fmt):
    g, _, n = scales.shape
    words = np.ascontiguousarray(words).reshape(g, 128, n, -1)
    if fmt == "e4m3":
        vals = words.view(ml_dtypes.float8_e4m3fn).astype(np.float64)
    else:
        nib = np.empty((g, 128, n, 4), np.uint8)
        nib[..., 0::2] = words & 0xF
        nib[..., 1::2] = words >> 4
        vals = E2M1[nib]
    vals = vals * np.repeat(np.exp2(scales.astype(np.float64) - 127.0), 8, axis=1)[..., None]
    return vals.transpose(0, 1, 3, 2).reshape(g * 512, n)


def gelu(v):
    return 0.5 * v * (1.0 + np.tanh(np.sqrt(2.0 / np.pi) * (v + 0.044715 * v**3)))


K, T, S, P, H, N = 1024, 2048, 1024, 512, 1024, 512

def setup_inputs():
    n = np.random.standard_normal
    s = mx_kscale(K)[:, None]
    u = mx_kscale(H)[:, None]
    tab_words, tab_scales = pack_weight(n((K, T)) * s, "e4m3")
    w1 = (n((K, H)) / np.sqrt(K) / s).astype(np.float32)
    gain = (np.exp(0.3 * n(H)) * u[:, 0]).astype(np.float32)
    w4_words, w4_scales = pack_weight(2.0 * n((H, N)) / np.sqrt(H) / u, "e2m1")
    return {
        "tab_words": tab_words, "tab_scales": tab_scales,
        "offs": striped(np.random.permutation(T)[:S]),
        "pos1": striped(np.random.permutation(S)[:P]),
        "pos2": striped(np.random.permutation(S)[:P]),
        "w1": w1, "gain": gain,
        "w4_words": w4_words, "w4_scales": w4_scales,
    }

def reference(tab_words, tab_scales, offs, pos1, pos2, w1, gain, w4_words, w4_scales):
    v = unpack_weight(tab_words, tab_scales, "e4m3")[:, unstriped(offs)]
    h = mxq(f64(w1), 0, "e4m3").T @ v
    a = h[:, unstriped(pos1)]
    b = h[:, unstriped(pos2)]
    z = f64(gain)[:, None] * (a / (1.0 + np.square(b)))
    w4 = unpack_weight(w4_words, w4_scales, "e2m1")
    y = w4.T @ mxq(z, 0, "e4m3")
    return 1.0 / (1.0 + np.exp(-y))

@@ -1,0 +1,306 @@
+from contextlib import ExitStack
+
+import concourse.mybir as mybir
+
+K, T, S, NP, H, N = 1024, 2048, 1024, 512, 1024, 512
+FLOPS = 2 * K * H * S + 2 * H * N * NP
+
+F32 = mybir.dt.float32
+BF16 = mybir.dt.bfloat16
+I32 = mybir.dt.int32
+U32 = mybir.dt.uint32
+U16 = mybir.dt.uint16
+U8 = mybir.dt.uint8
+FP8X4 = mybir.dt.float8_e4m3fn_x4
+FP4X4 = mybir.dt.float4_e2m1fn_x4
+ACT = mybir.ActivationFunctionType
+MULT = mybir.AluOpType.mult
+
+P = 128
+PACK = 4
+PASS = P * PACK
+BANK = 512
+PIECE = 256
+
+
+def tile_list_variant_pathogenicity_score_kernel(
+    tc, tab_words, tab_scales, offs, pos1, pos2, w1, gain, w4_words, w4_scales, out
+):
+    nc = tc.nc
+    with ExitStack() as ctx:
+        keep = ctx.enter_context(tc.tile_pool(name="keep", bufs=1))
+        ring = ctx.enter_context(tc.tile_pool(name="ring", bufs=4))
+        psum = ctx.enter_context(tc.psum_pool(name="psum", bufs=8))
+
+        def held(shape, dtype, name):
+            return keep.tile(shape, dtype, name=name, align_bytes=64)
+
+        offs_sb = keep.tile([P, S // 16], U16, name="offs_sb")
+        pos1_sb = keep.tile([P, NP // 16], U16, name="pos1_sb")
+        pos2_sb = keep.tile([P, NP // 16], U16, name="pos2_sb")
+        tab_s = held([P, T // 4], I32, "tab_s")
+        tab_w = [held([P, T], I32, "tab_w%d" % a) for a in range(2)]
+        w4_s = held([P, 2 * N // 4], I32, "w4_s")
+        w4_w = held([P, 2, 2 * N], U8, "w4_w")
+        gain_sb = held([P, 2, PACK], F32, "gain_sb")
+        w1_raw = {}
+        for g in range(2):
+            for a in range(2):
+                for mh in range(2):
+                    w1_raw[g, a, mh] = held([P, PACK, PIECE], F32, "w1_raw%d%d%d" % (g, a, mh))
+
+        one = held([P, 1], F32, "one")
+        warm = held([P, 1], F32, "warm")
+        nc.vector.memset(tab_s[:], 0)
+        nc.vector.memset(one[:], 1.0)
+        nc.scalar.activation(warm[:], one[:], ACT.Abs_reciprocal_sqrt)
+        nc.vector.memset(w4_s[:], 0)
+
+        def load_w1(g, a, mh):
+            c0 = g * PASS + mh * PIECE
+            src = w1[a * PASS : (a + 1) * PASS, c0 : c0 + PIECE]
+            nc.sync.dma_start(w1_raw[g, a, mh][:], src.rearrange("(p j) c -> p j c", j=PACK))
+
+        nc.sync.dma_start(offs_sb[:], offs)
+        tab_s_words = tab_scales.bitcast(I32)
+        for q in range(4):
+            nc.sync.dma_start(tab_s[32 * q : 32 * q + 8, :], tab_s_words[:, 4 * q : 4 * q + 4, :])
+        for a in range(2):
+            nc.sync.dma_start(tab_w[a][:], tab_words[a].rearrange("p t i -> p (t i)").bitcast(I32))
+            for mh in range(2):
+                load_w1(0, a, mh)
+        nc.sync.dma_start(pos2_sb[:], pos2)
+        nc.sync.dma_start(pos1_sb[:], pos1)
+        nc.sync.dma_start(gain_sb[:], gain.rearrange("(a p t) -> p a t", a=2, t=PACK))
+        for a in range(2):
+            for mh in range(2):
+                load_w1(1, a, mh)
+        nc.sync.dma_start(w4_w[:].bitcast(I32), w4_words.rearrange("a p c -> p a c").bitcast(I32))
+        w4_s_words = w4_scales.bitcast(I32)
+        for q in range(4):
+            nc.sync.dma_start(
+                w4_s[32 * q : 32 * q + 4, :].rearrange("r (a c) -> r a c", a=2),
+                w4_s_words[:, 4 * q : 4 * q + 4, :].rearrange("a r c -> r a c"),
+            )
+
+        v_s = held([P, S], U8, "v_s")
+        v_w = [held([P, S], U32, "v_w%d" % a) for a in range(2)]
+        halves = [slice(0, BANK), slice(BANK, 2 * BANK)]
+
+        def entries(lst, cols):
+            return lst[:, cols.start // 16 : cols.stop // 16]
+
+        for hf in halves:
+            nc.vector.tensor_copy(v_s[:, hf], tab_s[:].bitcast(U8).indirect(entries(offs_sb, hf)))
+
+        def pick_words(a):
+            for hf in halves:
+                nc.vector.tensor_copy(v_w[a][:, hf], tab_w[a][:].bitcast(U32).indirect(entries(offs_sb, hf)))
+
+        w1_bf = {}
+        w1_w = {}
+        w1_s = {}
+        for g in range(2):
+            for a in range(2):
+                w1_bf[g, a] = held([P, PACK, P, PACK], BF16, "w1_bf%d%d" % (g, a))
+                w1_w[g, a] = held([P, PASS], U32, "w1_w%d%d" % (g, a))
+                w1_s[g, a] = held([P, PASS], U8, "w1_s%d%d" % (g, a))
+
+        def round_w1(copy, g, a, mh, m0, m1):
+            src = w1_raw[g, a, mh][:].rearrange("p j (m t) -> p m j t", t=PACK)[:, m0:m1]
+            base = mh * (PIECE // PACK)
+            dst = w1_bf[g, a][:].rearrange("p t m j -> p m j t")[:, base + m0 : base + m1]
+            copy(dst, src)
+
+        def quantize_w1(g, a, t0, t1):
+            cols = slice(t0 * P, t1 * P)
+            nc.vector.quantize_mx(
+                out=w1_w[g, a][:, cols].bitcast(FP8X4),
+                scales=w1_s[g, a][:, cols],
+                in_=w1_bf[g, a][:, t0:t1].rearrange("p t m j -> p (t m j)"),
+            )
+
+        h = [keep.tile([P, S], F32, name="h%d" % i) for i in range(8)]
+        h_bank = {}
+
+        def h_pass(i, a):
+            g, t = divmod(i, PACK)
+            cols = slice(t * P, (t + 1) * P)
+            for u, hf in enumerate(halves):
+                if a == 0:
+                    h_bank[i, u] = psum.tile([P, BANK], F32, name="bank")
+                nc.tensor.matmul_mx(
+                    out=h_bank[i, u][:],
+                    lhsT=w1_w[g, a][:, cols].bitcast(FP8X4),
+                    lhsT_scale=w1_s[g, a][:, cols],
+                    rhs=v_w[a][:, hf].bitcast(FP8X4),
+                    rhs_scale=v_s[4 * a : P, hf],
+                    start=(a == 0),
+                    stop=(a == 1),
+                )
+
+        def h_out(i, copy0=nc.scalar.copy, copy1=nc.scalar.copy):
+            copy0(h[i][:, halves[0]], h_bank[i, 0][:])
+            copy1(h[i][:, halves[1]], h_bank[i, 1][:])
+
+        ref = {}
+        inv = {}
+        damp = [keep.tile([P, NP], F32, name="damp%d" % i) for i in range(8)]
+        z = [keep.tile([P, PACK, NP], F32, name="z%d" % g) for g in range(2)]
+        z_bf = [held([P, NP, PACK], BF16, "z_bf%d" % g) for g in range(2)]
+        z_w = [held([P, NP], U32, "z_w%d" % g) for g in range(2)]
+        z_s = [held([P, NP], U8, "z_s%d" % g) for g in range(2)]
+
+        def pick_ref(i):
+            ref[i] = ring.tile([P, NP], F32, name="ref")
+            nc.vector.tensor_copy(ref[i][:], h[i][:].indirect(pos2_sb[:]))
+
+        def inv_root(i):
+            sq = ring.tile([P, NP], F32, name="sq")
+            nc.scalar.activation(sq[:], ref[i][:], ACT.Square)
+            inv[i] = ring.tile([P, NP], F32, name="inv")
+            nc.scalar.activation(inv[i][:], sq[:], ACT.Abs_reciprocal_sqrt, bias=1.0)
+
+        def make_damp(i):
+            g, t = divmod(i, PACK)
+            nc.vector.scalar_tensor_tensor(damp[i][:], inv[i][:], gain_sb[:, g, t : t + 1], inv[i][:], MULT, MULT)
+
+        def pick_var(i, cols):
+            g, t = divmod(i, PACK)
+            nc.vector.tensor_tensor(z[g][:, t, cols], h[i][:].indirect(entries(pos1_sb, cols)), damp[i][:, cols], MULT)
+
+        def round_z(copy, g, cols):
+            copy(
+                z_bf[g][:, cols, :].rearrange("p (c i) t -> p c t i", i=4),
+                z[g][:, :, cols].rearrange("p t (c i) -> p c t i", i=4),
+            )
+
+        def quantize_z(g, cols):
+            nc.vector.quantize_mx(
+                out=z_w[g][:, cols].bitcast(FP8X4),
+                scales=z_s[g][:, cols],
+                in_=z_bf[g][:, cols, :].rearrange("p j t -> p (j t)"),
+            )
+
+        w4_s8 = w4_s[:].bitcast(U8)
+
+        def y_pass(dst, nt, g, cols):
+            nc.tensor.matmul_mx(
+                out=dst,
+                lhsT=w4_w[:, g, 2 * P * nt : 2 * P * (nt + 1)].bitcast(FP4X4),
+                lhsT_scale=w4_s8[:, g * N + P * nt : g * N + P * (nt + 1)],
+                rhs=z_w[g][:, cols].bitcast(FP8X4),
+                rhs_scale=z_s[g][:, cols],
+                start=(g == 0),
+                stop=(g == 1),
+            )
+
+        out_v = out.rearrange("(nt p) j -> p nt j", p=P)
+        res = held([P, PACK, PACK, P], F32, "res")
+
+        def score_block(b):
+            cols = slice(b * P, (b + 1) * P)
+            bank = psum.tile([P, PACK, P], F32, name="bank")
+            for nt in range(PACK):
+                for g in range(2):
+                    y_pass(bank[:, nt, :], nt, g, cols)
+            nc.scalar.activation(res[:, b], bank[:], ACT.Sigmoid)
+            nc.sync.dma_start(out_v[:, :, cols], res[:, b])
+
+        S_, V_ = nc.scalar.copy, nc.vector.tensor_copy
+        M_HALF = PIECE // PACK
+
+        pick_words(0)
+        round_w1(S_, 0, 0, 0, 0, M_HALF)
+        round_w1(S_, 0, 0, 1, 0, 24)
+        round_w1(V_, 0, 0, 1, 24, M_HALF)
+        quantize_w1(0, 0, 0, 4)
+        pick_words(1)
+        round_w1(S_, 0, 1, 0, 0, M_HALF)
+        round_w1(S_, 0, 1, 1, 0, 16)
+        round_w1(V_, 0, 1, 1, 16, M_HALF)
+        for t in range(PACK):
+            quantize_w1(0, 1, t, t + 1)
+        for i in range(4):
+            h_pass(i, 0)
+            h_pass(i, 1)
+
+        every = slice(0, NP)
+        h_out(0, S_, V_)
+        h_out(1)
+        pick_ref(0)
+        round_w1(V_, 1, 0, 0, 0, M_HALF)
+        inv_root(0)
+        pick_ref(1)
+        h_out(2)
+        round_w1(S_, 1, 0, 1, 0, M_HALF)
+        make_damp(0)
+        inv_root(1)
+        pick_ref(2)
+        pick_var(0, every)
+        h_out(3)
+        quantize_w1(1, 0, 0, 4)
+        round_w1(S_, 1, 1, 0, 0, M_HALF)
+        make_damp(1)
+        pick_ref(3)
+        inv_root(2)
+        round_w1(S_, 1, 1, 1, 0, M_HALF)
+        pick_var(1, every)
+        quantize_w1(1, 1, 0, 4)
+        for i in range(4, 8):
+            h_pass(i, 0)
+            h_pass(i, 1)
+        inv_root(3)
+        make_damp(2)
+        h_out(4)
+        pick_var(2, every)
+        make_damp(3)
+        pick_ref(4)
+        h_out(5)
+        inv_root(4)
+        pick_var(3, every)
+        pick_ref(5)
+        h_out(6)
+        inv_root(5)
+        make_damp(4)
+        pick_ref(6)
+        h_out(7)
+        inv_root(6)
+        make_damp(5)
+        pick_ref(7)
+        inv_root(7)
+        round_z(S_, 0, every)
+        make_damp(6)
+        first = slice(0, 2 * P)
+        pick_var(4, first)
+        pick_var(5, first)
+        make_damp(7)
+        pick_var(6, first)
+        quantize_z(0, every)
+        second = slice(2 * P, 3 * P)
+        last = slice(3 * P, 4 * P)
+        last_banks = [psum.tile([P, P], F32, name="bank") for nt in range(PACK)]
+        for nt in range(PACK):
+            y_pass(last_banks[nt][:], nt, 0, last)
+        pick_var(7, first)
+        round_z(S_, 1, first)
+        pick_var(4, second)
+        pick_var(5, second)
+        quantize_z(1, first)
+        score_block(0)
+        score_block(1)
+        pick_var(6, second)
+        pick_var(7, second)
+        pick_var(4, last)
+        round_z(V_, 1, second)
+        pick_var(5, last)
+        quantize_z(1, second)
+        score_block(2)
+        pick_var(6, last)
+        pick_var(7, last)
+        round_z(V_, 1, last)
+        quantize_z(1, last)
+        for nt in range(PACK):
+            y_pass(last_banks[nt][:], nt, 1, last)
+            nc.scalar.activation(res[:, 3, nt], last_banks[nt][:], ACT.Sigmoid)
+            nc.sync.dma_start(out_v[:, nt, last], res[:, 3, nt])

@@ -15,12 +15,12 @@ FP8X4 = mybir.dt.float8_e4m3fn_x4
 FP4X4 = mybir.dt.float4_e2m1fn_x4
 ACT = mybir.ActivationFunctionType
 MULT = mybir.AluOpType.mult
+ADD = mybir.AluOpType.add
 
 P = 128
 PACK = 4
 PASS = P * PACK
 BANK = 512
-PIECE = 256
 
 
 def tile_list_variant_pathogenicity_score_kernel(
@@ -29,7 +29,6 @@ def tile_list_variant_pathogenicity_score_kernel(
     nc = tc.nc
     with ExitStack() as ctx:
         keep = ctx.enter_context(tc.tile_pool(name="keep", bufs=1))
-        ring = ctx.enter_context(tc.tile_pool(name="ring", bufs=4))
         psum = ctx.enter_context(tc.psum_pool(name="psum", bufs=8))
 
         def held(shape, dtype, name):
@@ -43,38 +42,39 @@ def tile_list_variant_pathogenicity_score_kernel(
         w4_s = held([P, 2 * N // 4], I32, "w4_s")
         w4_w = held([P, 2, 2 * N], U8, "w4_w")
         gain_sb = held([P, 2, PACK], F32, "gain_sb")
-        w1_raw = {}
-        for g in range(2):
-            for a in range(2):
-                for mh in range(2):
-                    w1_raw[g, a, mh] = held([P, PACK, PIECE], F32, "w1_raw%d%d%d" % (g, a, mh))
 
         one = held([P, 1], F32, "one")
         warm = held([P, 1], F32, "warm")
         nc.vector.memset(tab_s[:], 0)
         nc.vector.memset(one[:], 1.0)
         nc.scalar.activation(warm[:], one[:], ACT.Abs_reciprocal_sqrt)
-        nc.vector.memset(w4_s[:], 0)
+        nc.gpsimd.memset(w4_s[:], 0)
 
-        def load_w1(g, a, mh):
-            c0 = g * PASS + mh * PIECE
-            src = w1[a * PASS : (a + 1) * PASS, c0 : c0 + PIECE]
-            nc.sync.dma_start(w1_raw[g, a, mh][:], src.rearrange("(p j) c -> p j c", j=PACK))
+        w1_raw = {}
+
+        def load_w1(g, a, c0, c1):
+            w1_raw[g, a, c0] = held([P, PACK, c1 - c0], F32, "w1_raw%d%d_%d" % (g, a, c0))
+            src = w1[a * PASS : (a + 1) * PASS, g * PASS + c0 : g * PASS + c1]
+            nc.sync.dma_start(w1_raw[g, a, c0][:], src.rearrange("(p j) c -> p j c", j=PACK))
+
+        def load_words(a):
+            nc.sync.dma_start(tab_w[a][:], tab_words[a].rearrange("p t i -> p (t i)").bitcast(I32))
 
         nc.sync.dma_start(offs_sb[:], offs)
+        load_words(0)
         tab_s_words = tab_scales.bitcast(I32)
         for q in range(4):
             nc.sync.dma_start(tab_s[32 * q : 32 * q + 8, :], tab_s_words[:, 4 * q : 4 * q + 4, :])
-        for a in range(2):
-            nc.sync.dma_start(tab_w[a][:], tab_words[a].rearrange("p t i -> p (t i)").bitcast(I32))
-            for mh in range(2):
-                load_w1(0, a, mh)
+        load_w1(0, 0, 0, 256)
         nc.sync.dma_start(pos2_sb[:], pos2)
         nc.sync.dma_start(pos1_sb[:], pos1)
+        load_w1(0, 0, 256, 512)
+        load_words(1)
+        load_w1(0, 1, 0, 256)
+        load_w1(0, 1, 256, 512)
+        load_w1(1, 0, 0, 512)
+        load_w1(1, 1, 0, 512)
         nc.sync.dma_start(gain_sb[:], gain.rearrange("(a p t) -> p a t", a=2, t=PACK))
-        for a in range(2):
-            for mh in range(2):
-                load_w1(1, a, mh)
         nc.sync.dma_start(w4_w[:].bitcast(I32), w4_words.rearrange("a p c -> p a c").bitcast(I32))
         w4_s_words = w4_scales.bitcast(I32)
         for q in range(4):
@@ -87,29 +87,25 @@ def tile_list_variant_pathogenicity_score_kernel(
         v_w = [held([P, S], U32, "v_w%d" % a) for a in range(2)]
         halves = [slice(0, BANK), slice(BANK, 2 * BANK)]
 
-        def entries(lst, cols):
-            return lst[:, cols.start // 16 : cols.stop // 16]
-
-        for hf in halves:
-            nc.vector.tensor_copy(v_s[:, hf], tab_s[:].bitcast(U8).indirect(entries(offs_sb, hf)))
-
         def pick_words(a):
-            for hf in halves:
-                nc.vector.tensor_copy(v_w[a][:, hf], tab_w[a][:].bitcast(U32).indirect(entries(offs_sb, hf)))
+            nc.vector.tensor_copy(v_w[a][:], tab_w[a][:].bitcast(U32).indirect(offs_sb[:]))
+
+        def pick_scales():
+            nc.vector.tensor_copy(v_s[:], tab_s[:].bitcast(U8).indirect(offs_sb[:]))
 
         w1_bf = {}
         w1_w = {}
         w1_s = {}
         for g in range(2):
             for a in range(2):
-                w1_bf[g, a] = held([P, PACK, P, PACK], BF16, "w1_bf%d%d" % (g, a))
+                if g == 0:
+                    w1_bf[g, a] = held([P, PACK, P, PACK], BF16, "w1_bf%d%d" % (g, a))
                 w1_w[g, a] = held([P, PASS], U32, "w1_w%d%d" % (g, a))
                 w1_s[g, a] = held([P, PASS], U8, "w1_s%d%d" % (g, a))
 
-        def round_w1(copy, g, a, mh, m0, m1):
-            src = w1_raw[g, a, mh][:].rearrange("p j (m t) -> p m j t", t=PACK)[:, m0:m1]
-            base = mh * (PIECE // PACK)
-            dst = w1_bf[g, a][:].rearrange("p t m j -> p m j t")[:, base + m0 : base + m1]
+        def round_w1(copy, g, a, c0, m0, m1):
+            src = w1_raw[g, a, c0][:].rearrange("p j (m t) -> p m j t", t=PACK)[:, m0 - c0 // PACK : m1 - c0 // PACK]
+            dst = w1_bf[g, a][:].rearrange("p t m j -> p m j t")[:, m0:m1]
             copy(dst, src)
 
         def quantize_w1(g, a, t0, t1):
@@ -143,36 +139,59 @@ def tile_list_variant_pathogenicity_score_kernel(
             copy0(h[i][:, halves[0]], h_bank[i, 0][:])
             copy1(h[i][:, halves[1]], h_bank[i, 1][:])
 
-        ref = {}
-        inv = {}
-        damp = [keep.tile([P, NP], F32, name="damp%d" % i) for i in range(8)]
-        z = [keep.tile([P, PACK, NP], F32, name="z%d" % g) for g in range(2)]
+        var_rows = held([P, PACK + 2, NP], F32, "var_rows")
+        var = [var_rows[:, 0:PACK], var_rows[:, 2 : PACK + 2]]
+        damp = [held([P, PACK, NP], F32, "damp%d" % g) for g in range(2)]
         z_bf = [held([P, NP, PACK], BF16, "z_bf%d" % g) for g in range(2)]
         z_w = [held([P, NP], U32, "z_w%d" % g) for g in range(2)]
         z_s = [held([P, NP], U8, "z_s%d" % g) for g in range(2)]
 
+        def row(tiles, i):
+            return tiles[i // PACK][:, i % PACK, :]
+
         def pick_ref(i):
-            ref[i] = ring.tile([P, NP], F32, name="ref")
-            nc.vector.tensor_copy(ref[i][:], h[i][:].indirect(pos2_sb[:]))
+            nc.vector.tensor_copy(row(damp, i), h[i][:].indirect(pos2_sb[:]))
+
+        def pick_var(i):
+            nc.vector.tensor_copy(row(var, i), h[i][:].indirect(pos1_sb[:]))
+
+        def square(i):
+            nc.scalar.activation(row(damp, i), row(damp, i), ACT.Square)
+
+        def square_pool(i):
+            nc.gpsimd.tensor_tensor(row(damp, i), row(damp, i), row(damp, i), MULT)
 
         def inv_root(i):
-            sq = ring.tile([P, NP], F32, name="sq")
-            nc.scalar.activation(sq[:], ref[i][:], ACT.Square)
-            inv[i] = ring.tile([P, NP], F32, name="inv")
-            nc.scalar.activation(inv[i][:], sq[:], ACT.Abs_reciprocal_sqrt, bias=1.0)
+            nc.scalar.activation(row(damp, i), row(damp, i), ACT.Abs_reciprocal_sqrt, bias=1.0)
+
+        def scale_by_gain(i):
+            g, t = divmod(i, PACK)
+            nc.gpsimd.tensor_scalar(row(damp, i), row(damp, i), gain_sb[:, g, t : t + 1], 0.0, MULT, ADD)
+
+        zf = [held([P, PACK, NP], F32, "zf%d" % g) for g in range(2)]
+
+        def entries(lst, cols):
+            return lst[:, cols.start // 16 : cols.stop // 16]
 
         def make_damp(i):
             g, t = divmod(i, PACK)
-            nc.vector.scalar_tensor_tensor(damp[i][:], inv[i][:], gain_sb[:, g, t : t + 1], inv[i][:], MULT, MULT)
+            nc.vector.scalar_tensor_tensor(row(damp, i), row(damp, i), gain_sb[:, g, t : t + 1], row(damp, i), MULT, MULT)
 
-        def pick_var(i, cols):
-            g, t = divmod(i, PACK)
-            nc.vector.tensor_tensor(z[g][:, t, cols], h[i][:].indirect(entries(pos1_sb, cols)), damp[i][:, cols], MULT)
+        def pick_damped(i, cols):
+            nc.vector.tensor_tensor(row(zf, i)[:, cols], h[i][:].indirect(entries(pos1_sb, cols)), row(damp, i)[:, cols], MULT)
 
         def round_z(copy, g, cols):
             copy(
                 z_bf[g][:, cols, :].rearrange("p (c i) t -> p c t i", i=4),
-                z[g][:, :, cols].rearrange("p t (c i) -> p c t i", i=4),
+                zf[g][:, :, cols].rearrange("p t (c i) -> p c t i", i=4),
+            )
+
+        def make_z(g, cols):
+            nc.vector.tensor_tensor(
+                z_bf[g][:, cols, :].rearrange("p (c i) t -> p c t i", i=4),
+                var[g][:, :, cols].rearrange("p t (c i) -> p c t i", i=4),
+                damp[g][:, :, cols].rearrange("p t (c i) -> p c t i", i=4),
+                MULT,
             )
 
         def quantize_z(g, cols):
@@ -184,123 +203,122 @@ def tile_list_variant_pathogenicity_score_kernel(
 
         w4_s8 = w4_s[:].bitcast(U8)
 
-        def y_pass(dst, nt, g, cols):
+        def y_pass(dst, nt, g, cols, start, stop):
             nc.tensor.matmul_mx(
                 out=dst,
                 lhsT=w4_w[:, g, 2 * P * nt : 2 * P * (nt + 1)].bitcast(FP4X4),
                 lhsT_scale=w4_s8[:, g * N + P * nt : g * N + P * (nt + 1)],
                 rhs=z_w[g][:, cols].bitcast(FP8X4),
                 rhs_scale=z_s[g][:, cols],
-                start=(g == 0),
-                stop=(g == 1),
+                start=start,
+                stop=stop,
             )
 
         out_v = out.rearrange("(nt p) j -> p nt j", p=P)
         res = held([P, PACK, PACK, P], F32, "res")
+        y_bank = {}
 
-        def score_block(b):
+        def open_block(b, n0, n1, tag):
+            y_bank[b, n0] = psum.tile([P, n1 - n0, P], F32, name=tag)
+            for nt in range(n0, n1):
+                y_pass(y_bank[b, n0][:, nt - n0, :], nt, 0, slice(b * P, (b + 1) * P), nt == n0, False)
+
+        def close_block(b, n0, n1):
             cols = slice(b * P, (b + 1) * P)
-            bank = psum.tile([P, PACK, P], F32, name="bank")
-            for nt in range(PACK):
-                for g in range(2):
-                    y_pass(bank[:, nt, :], nt, g, cols)
-            nc.scalar.activation(res[:, b], bank[:], ACT.Sigmoid)
-            nc.sync.dma_start(out_v[:, :, cols], res[:, b])
+            for nt in range(n0, n1):
+                y_pass(y_bank[b, n0][:, nt - n0, :], nt, 1, cols, False, nt == n1 - 1)
+            nc.scalar.activation(res[:, b, n0:n1], y_bank[b, n0][:], ACT.Sigmoid)
+            nc.sync.dma_start(out_v[:, n0:n1, cols], res[:, b, n0:n1])
 
         S_, V_ = nc.scalar.copy, nc.vector.tensor_copy
-        M_HALF = PIECE // PACK
 
         pick_words(0)
-        round_w1(S_, 0, 0, 0, 0, M_HALF)
-        round_w1(S_, 0, 0, 1, 0, 24)
-        round_w1(V_, 0, 0, 1, 24, M_HALF)
+        pick_scales()
+        round_w1(S_, 0, 0, 0, 0, 64)
+        round_w1(S_, 0, 0, 256, 64, 128)
         quantize_w1(0, 0, 0, 4)
         pick_words(1)
-        round_w1(S_, 0, 1, 0, 0, M_HALF)
-        round_w1(S_, 0, 1, 1, 0, 16)
-        round_w1(V_, 0, 1, 1, 16, M_HALF)
-        for t in range(PACK):
-            quantize_w1(0, 1, t, t + 1)
+        round_w1(S_, 0, 1, 0, 0, 64)
+        round_w1(S_, 0, 1, 256, 64, 84)
+        round_w1(V_, 0, 1, 256, 84, 128)
+        quantize_w1(0, 1, 0, 1)
+        quantize_w1(0, 1, 1, 2)
+        quantize_w1(0, 1, 2, 4)
         for i in range(4):
             h_pass(i, 0)
             h_pass(i, 1)
 
-        every = slice(0, NP)
+        w1_bf[1, 0] = held([P, PACK, P, PACK], BF16, "w1_w01")
+        w1_bf[1, 1] = held([P, PACK, P, PACK], BF16, "w1_bf00")
         h_out(0, S_, V_)
-        h_out(1)
         pick_ref(0)
-        round_w1(V_, 1, 0, 0, 0, M_HALF)
-        inv_root(0)
+        pick_var(0)
+        square_pool(0)
+        h_out(1)
         pick_ref(1)
-        h_out(2)
-        round_w1(S_, 1, 0, 1, 0, M_HALF)
-        make_damp(0)
-        inv_root(1)
-        pick_ref(2)
-        pick_var(0, every)
-        h_out(3)
+        pick_var(1)
+        square_pool(1)
+        round_w1(S_, 1, 0, 0, 0, 128)
         quantize_w1(1, 0, 0, 4)
-        round_w1(S_, 1, 1, 0, 0, M_HALF)
-        make_damp(1)
-        pick_ref(3)
-        inv_root(2)
-        round_w1(S_, 1, 1, 1, 0, M_HALF)
-        pick_var(1, every)
+        h_out(2)
+        pick_ref(2)
+        pick_var(2)
+        square_pool(2)
+        round_w1(S_, 1, 1, 0, 0, 128)
         quantize_w1(1, 1, 0, 4)
-        for i in range(4, 8):
+        h_out(3)
+        pick_ref(3)
+        pick_var(3)
+        square_pool(3)
+
+        order = (6, 7, 4, 5)
+        for i in order:
             h_pass(i, 0)
             h_pass(i, 1)
-        inv_root(3)
-        make_damp(2)
-        h_out(4)
-        pick_var(2, every)
-        make_damp(3)
-        pick_ref(4)
-        h_out(5)
-        inv_root(4)
-        pick_var(3, every)
-        pick_ref(5)
-        h_out(6)
-        inv_root(5)
-        make_damp(4)
-        pick_ref(6)
-        h_out(7)
-        inv_root(6)
-        make_damp(5)
-        pick_ref(7)
-        inv_root(7)
-        round_z(S_, 0, every)
-        make_damp(6)
-        first = slice(0, 2 * P)
-        pick_var(4, first)
-        pick_var(5, first)
-        make_damp(7)
-        pick_var(6, first)
-        quantize_z(0, every)
-        second = slice(2 * P, 3 * P)
-        last = slice(3 * P, 4 * P)
-        last_banks = [psum.tile([P, P], F32, name="bank") for nt in range(PACK)]
-        for nt in range(PACK):
-            y_pass(last_banks[nt][:], nt, 0, last)
-        pick_var(7, first)
-        round_z(S_, 1, first)
-        pick_var(4, second)
-        pick_var(5, second)
-        quantize_z(1, first)
-        score_block(0)
-        score_block(1)
-        pick_var(6, second)
-        pick_var(7, second)
-        pick_var(4, last)
-        round_z(V_, 1, second)
-        pick_var(5, last)
-        quantize_z(1, second)
-        score_block(2)
-        pick_var(6, last)
-        pick_var(7, last)
-        round_z(V_, 1, last)
-        quantize_z(1, last)
-        for nt in range(PACK):
-            y_pass(last_banks[nt][:], nt, 1, last)
-            nc.scalar.activation(res[:, 3, nt], last_banks[nt][:], ACT.Sigmoid)
-            nc.sync.dma_start(out_v[:, nt, last], res[:, 3, nt])
+        inv_root(0)
+        inv_root(1)
+        square(0)
+        for n, i in enumerate(order):
+            h_out(i)
+            pick_ref(i)
+            if n < 2:
+                pick_var(i)
+                square_pool(i)
+            if n == 0:
+                square(1)
+                scale_by_gain(0)
+                scale_by_gain(1)
+            elif n == 1:
+                inv_root(2)
+                square(2)
+                scale_by_gain(2)
+            elif n == 2:
+                inv_root(3)
+        square(3)
+        scale_by_gain(3)
+        make_z(0, slice(0, NP))
+        for n, i in enumerate(order):
+            if n >= 2:
+                square(i)
+            inv_root(i)
+            square(i)
+            scale_by_gain(i)
+        pick_var(4)
+        quantize_z(0, slice(0, NP))
+        pick_var(5)
+
+        for b in range(3):
+            open_block(b, 0, 4, "bank")
+        open_block(3, 0, 2, "bank")
+        open_block(3, 2, 4, "bank")
+        make_z(1, slice(0, 256))
+        make_z(1, slice(256, 384))
+        quantize_z(1, slice(0, 256))
+        close_block(0, 0, 4)
+        close_block(1, 0, 4)
+        make_z(1, slice(384, 512))
+        quantize_z(1, slice(256, 384))
+        close_block(2, 0, 4)
+        quantize_z(1, slice(384, 512))
+        close_block(3, 0, 2)
+        close_block(3, 2, 4)

@@ -139,66 +139,62 @@ def tile_list_variant_pathogenicity_score_kernel(
             copy0(h[i][:, halves[0]], h_bank[i, 0][:])
             copy1(h[i][:, halves[1]], h_bank[i, 1][:])
 
-        var_rows = held([P, PACK + 2, NP], F32, "var_rows")
-        var = [var_rows[:, 0:PACK], var_rows[:, 2 : PACK + 2]]
+        var = [held([P, PACK, NP], F32, "var%d" % g) for g in range(2)]
         damp = [held([P, PACK, NP], F32, "damp%d" % g) for g in range(2)]
-        z_bf = [held([P, NP, PACK], BF16, "z_bf%d" % g) for g in range(2)]
         z_w = [held([P, NP], U32, "z_w%d" % g) for g in range(2)]
         z_s = [held([P, NP], U8, "z_s%d" % g) for g in range(2)]
 
         def row(tiles, i):
             return tiles[i // PACK][:, i % PACK, :]
 
+        def ref(i):
+            return row(var, i + PACK) if i in (2, 3) else row(damp, i)
+
         def pick_ref(i):
-            nc.vector.tensor_copy(row(damp, i), h[i][:].indirect(pos2_sb[:]))
+            nc.vector.tensor_copy(ref(i), h[i][:].indirect(pos2_sb[:]))
 
         def pick_var(i):
             nc.vector.tensor_copy(row(var, i), h[i][:].indirect(pos1_sb[:]))
 
+        def square_ref(i):
+            nc.scalar.activation(ref(i), ref(i), ACT.Square)
+
+        def square_ref_pool(i):
+            nc.gpsimd.tensor_tensor(ref(i), ref(i), ref(i), MULT)
+
+        def inv_root(i):
+            nc.scalar.activation(row(damp, i), ref(i), ACT.Abs_reciprocal_sqrt, bias=1.0)
+
+        def scale_by_gain_scalar(i):
+            g, t = divmod(i, PACK)
+            nc.scalar.activation(row(var, i), row(var, i), ACT.Copy, scale=gain_sb[:, g, t : t + 1])
+
         def square(i):
             nc.scalar.activation(row(damp, i), row(damp, i), ACT.Square)
 
-        def square_pool(i):
-            nc.gpsimd.tensor_tensor(row(damp, i), row(damp, i), row(damp, i), MULT)
-
-        def inv_root(i):
-            nc.scalar.activation(row(damp, i), row(damp, i), ACT.Abs_reciprocal_sqrt, bias=1.0)
-
-        def scale_by_gain(i):
+        def scale_by_gain(engine, i):
             g, t = divmod(i, PACK)
-            nc.gpsimd.tensor_scalar(row(damp, i), row(damp, i), gain_sb[:, g, t : t + 1], 0.0, MULT, ADD)
+            engine.tensor_scalar(row(var, i), row(var, i), gain_sb[:, g, t : t + 1], 0.0, MULT, ADD)
 
-        zf = [held([P, PACK, NP], F32, "zf%d" % g) for g in range(2)]
+        z_bf = {}
 
-        def entries(lst, cols):
-            return lst[:, cols.start // 16 : cols.stop // 16]
-
-        def make_damp(i):
-            g, t = divmod(i, PACK)
-            nc.vector.scalar_tensor_tensor(row(damp, i), row(damp, i), gain_sb[:, g, t : t + 1], row(damp, i), MULT, MULT)
-
-        def pick_damped(i, cols):
-            nc.vector.tensor_tensor(row(zf, i)[:, cols], h[i][:].indirect(entries(pos1_sb, cols)), row(damp, i)[:, cols], MULT)
-
-        def round_z(copy, g, cols):
-            copy(
-                z_bf[g][:, cols, :].rearrange("p (c i) t -> p c t i", i=4),
-                zf[g][:, :, cols].rearrange("p t (c i) -> p c t i", i=4),
-            )
-
-        def make_z(g, cols):
+        def make_z(g, b):
+            cols = slice(b * P, (b + 1) * P)
+            if g == 0:
+                z_bf[b] = keep.tile([P, 2, P, PACK], BF16, name="z_bf", align_bytes=64, bufs=2)
             nc.vector.tensor_tensor(
-                z_bf[g][:, cols, :].rearrange("p (c i) t -> p c t i", i=4),
+                z_bf[b][:, g].rearrange("p (c i) t -> p c t i", i=4),
                 var[g][:, :, cols].rearrange("p t (c i) -> p c t i", i=4),
                 damp[g][:, :, cols].rearrange("p t (c i) -> p c t i", i=4),
                 MULT,
             )
 
-        def quantize_z(g, cols):
+        def quantize_z(g, b):
+            cols = slice(b * P, (b + 1) * P)
             nc.vector.quantize_mx(
                 out=z_w[g][:, cols].bitcast(FP8X4),
                 scales=z_s[g][:, cols],
-                in_=z_bf[g][:, cols, :].rearrange("p j t -> p (j t)"),
+                in_=z_bf[b][:, g].rearrange("p j t -> p (j t)"),
             )
 
         w4_s8 = w4_s[:].bitcast(U8)
@@ -250,75 +246,72 @@ def tile_list_variant_pathogenicity_score_kernel(
 
         w1_bf[1, 0] = held([P, PACK, P, PACK], BF16, "w1_w01")
         w1_bf[1, 1] = held([P, PACK, P, PACK], BF16, "w1_bf00")
-        h_out(0, S_, V_)
-        pick_ref(0)
-        pick_var(0)
-        square_pool(0)
-        h_out(1)
-        pick_ref(1)
-        pick_var(1)
-        square_pool(1)
-        round_w1(S_, 1, 0, 0, 0, 128)
-        quantize_w1(1, 0, 0, 4)
-        h_out(2)
-        pick_ref(2)
-        pick_var(2)
-        square_pool(2)
-        round_w1(S_, 1, 1, 0, 0, 128)
-        quantize_w1(1, 1, 0, 4)
-        h_out(3)
-        pick_ref(3)
-        pick_var(3)
-        square_pool(3)
-
-        order = (6, 7, 4, 5)
-        for i in order:
+        for i in range(4):
+            if i == 0:
+                h_out(0, S_, V_)
+            else:
+                h_out(i)
+            pick_ref(i)
+            pick_var(i)
+            square_ref_pool(i)
+            scale_by_gain(nc.gpsimd, i)
+            if i in (1, 2):
+                round_w1(S_, 1, i - 1, 0, 0, 128)
+                quantize_w1(1, i - 1, 0, 4)
+        for i in range(4, 8):
             h_pass(i, 0)
             h_pass(i, 1)
         inv_root(0)
         inv_root(1)
         square(0)
-        for n, i in enumerate(order):
+        for i in range(4, 8):
             h_out(i)
             pick_ref(i)
-            if n < 2:
+            square_ref_pool(i)
+            if i < 6:
                 pick_var(i)
-                square_pool(i)
-            if n == 0:
+                scale_by_gain(nc.gpsimd, i)
+            if i == 4:
                 square(1)
-                scale_by_gain(0)
-                scale_by_gain(1)
-            elif n == 1:
-                inv_root(2)
-                square(2)
-                scale_by_gain(2)
-            elif n == 2:
-                inv_root(3)
+        inv_root(2)
+        inv_root(3)
+        pick_var(6)
+        scale_by_gain(nc.gpsimd, 6)
+        pick_var(7)
+        square(2)
         square(3)
-        scale_by_gain(3)
-        make_z(0, slice(0, NP))
-        for n, i in enumerate(order):
-            if n >= 2:
-                square(i)
-            inv_root(i)
-            square(i)
-            scale_by_gain(i)
-        pick_var(4)
-        quantize_z(0, slice(0, NP))
-        pick_var(5)
-
-        for b in range(3):
-            open_block(b, 0, 4, "bank")
+        inv_root(4)
+        inv_root(5)
+        square(4)
+        square(5)
+        inv_root(6)
+        inv_root(7)
+        square(6)
+        square(7)
+        scale_by_gain_scalar(7)
+        make_z(0, 0)
+        make_z(0, 1)
+        quantize_z(0, 0)
+        open_block(0, 0, 4, "bank")
+        quantize_z(0, 1)
+        open_block(1, 0, 4, "bank")
+        make_z(1, 0)
+        make_z(1, 1)
+        quantize_z(1, 0)
+        close_block(0, 0, 4)
+        make_z(0, 2)
+        quantize_z(1, 1)
+        close_block(1, 0, 4)
+        make_z(1, 2)
+        quantize_z(0, 2)
+        open_block(2, 0, 4, "bank")
+        make_z(0, 3)
+        quantize_z(1, 2)
+        close_block(2, 0, 4)
+        quantize_z(0, 3)
         open_block(3, 0, 2, "bank")
         open_block(3, 2, 4, "bank")
-        make_z(1, slice(0, 256))
-        make_z(1, slice(256, 384))
-        quantize_z(1, slice(0, 256))
-        close_block(0, 0, 4)
-        close_block(1, 0, 4)
-        make_z(1, slice(384, 512))
-        quantize_z(1, slice(256, 384))
-        close_block(2, 0, 4)
-        quantize_z(1, slice(384, 512))
+        make_z(1, 3)
+        quantize_z(1, 3)
         close_block(3, 0, 2)
         close_block(3, 2, 4)

@@ -72,9 +72,10 @@ def tile_list_variant_pathogenicity_score_kernel(
         load_words(1)
         load_w1(0, 1, 0, 256)
         load_w1(0, 1, 256, 512)
-        load_w1(1, 0, 0, 512)
-        load_w1(1, 1, 0, 512)
+        load_w1(1, 0, 0, 256)
         nc.sync.dma_start(gain_sb[:], gain.rearrange("(a p t) -> p a t", a=2, t=PACK))
+        load_w1(1, 0, 256, 512)
+        load_w1(1, 1, 0, 512)
         nc.sync.dma_start(w4_w[:].bitcast(I32), w4_words.rearrange("a p c -> p a c").bitcast(I32))
         w4_s_words = w4_scales.bitcast(I32)
         for q in range(4):
@@ -100,8 +101,18 @@ def tile_list_variant_pathogenicity_score_kernel(
             for a in range(2):
                 if g == 0:
                     w1_bf[g, a] = held([P, PACK, P, PACK], BF16, "w1_bf%d%d" % (g, a))
-                w1_w[g, a] = held([P, PASS], U32, "w1_w%d%d" % (g, a))
+                if (g, a) == (0, 1):
+                    w1_w[g, a] = held([P, 2 * P], U32, "w1_w01")
+                else:
+                    w1_w[g, a] = held([P, PASS], U32, "w1_w%d%d" % (g, a))
                 w1_s[g, a] = held([P, PASS], U8, "w1_s%d%d" % (g, a))
+
+        w1_w_last = held([P, 2 * P], U32, "w1_w_last")
+
+        def w1_codes(g, a, t0, t1):
+            if (g, a) == (0, 1) and t0 >= 2:
+                return w1_w_last[:, (t0 - 2) * P : (t1 - 2) * P].bitcast(FP8X4)
+            return w1_w[g, a][:, t0 * P : t1 * P].bitcast(FP8X4)
 
         def round_w1(copy, g, a, c0, m0, m1):
             src = w1_raw[g, a, c0][:].rearrange("p j (m t) -> p m j t", t=PACK)[:, m0 - c0 // PACK : m1 - c0 // PACK]
@@ -111,12 +122,12 @@ def tile_list_variant_pathogenicity_score_kernel(
         def quantize_w1(g, a, t0, t1):
             cols = slice(t0 * P, t1 * P)
             nc.vector.quantize_mx(
-                out=w1_w[g, a][:, cols].bitcast(FP8X4),
+                out=w1_codes(g, a, t0, t1),
                 scales=w1_s[g, a][:, cols],
                 in_=w1_bf[g, a][:, t0:t1].rearrange("p t m j -> p (t m j)"),
             )
 
-        h = [keep.tile([P, S], F32, name="h%d" % i) for i in range(8)]
+        h = {i: held([P, S], F32, "h%d" % i) for i in range(8) if i != 3}
         h_bank = {}
 
         def h_pass(i, a):
@@ -127,13 +138,16 @@ def tile_list_variant_pathogenicity_score_kernel(
                     h_bank[i, u] = psum.tile([P, BANK], F32, name="bank")
                 nc.tensor.matmul_mx(
                     out=h_bank[i, u][:],
-                    lhsT=w1_w[g, a][:, cols].bitcast(FP8X4),
+                    lhsT=w1_codes(g, a, t, t + 1),
                     lhsT_scale=w1_s[g, a][:, cols],
                     rhs=v_w[a][:, hf].bitcast(FP8X4),
                     rhs_scale=v_s[4 * a : P, hf],
                     start=(a == 0),
                     stop=(a == 1),
                 )
+
+        def h_half(i, u):
+            nc.scalar.copy(h[i][:, halves[u]], h_bank[i, u][:])
 
         def h_out(i, copy0=nc.scalar.copy, copy1=nc.scalar.copy):
             copy0(h[i][:, halves[0]], h_bank[i, 0][:])
@@ -160,7 +174,12 @@ def tile_list_variant_pathogenicity_score_kernel(
             nc.scalar.activation(ref(i), ref(i), ACT.Square)
 
         def square_ref_pool(i):
-            nc.gpsimd.tensor_tensor(ref(i), ref(i), ref(i), MULT)
+            part = ref(i)[:, 0:SPLIT]
+            nc.gpsimd.tensor_tensor(part, part, part, MULT)
+
+        def square_ref_rest(i):
+            part = ref(i)[:, SPLIT:NP]
+            nc.scalar.activation(part, part, ACT.Square)
 
         def inv_root(i):
             nc.scalar.activation(row(damp, i), ref(i), ACT.Abs_reciprocal_sqrt, bias=1.0)
@@ -226,6 +245,7 @@ def tile_list_variant_pathogenicity_score_kernel(
             nc.scalar.activation(res[:, b, n0:n1], y_bank[b, n0][:], ACT.Sigmoid)
             nc.sync.dma_start(out_v[:, n0:n1, cols], res[:, b, n0:n1])
 
+        SPLIT = 256
         S_, V_ = nc.scalar.copy, nc.vector.tensor_copy
 
         pick_words(0)
@@ -245,51 +265,68 @@ def tile_list_variant_pathogenicity_score_kernel(
             h_pass(i, 1)
 
         w1_bf[1, 0] = held([P, PACK, P, PACK], BF16, "w1_w01")
-        w1_bf[1, 1] = held([P, PACK, P, PACK], BF16, "w1_bf00")
-        for i in range(4):
-            if i == 0:
-                h_out(0, S_, V_)
-            else:
-                h_out(i)
+        w1_bf[1, 1] = held([P, PACK, P, PACK], BF16, "w1_w_last")
+        def picks(i):
             pick_ref(i)
-            pick_var(i)
             square_ref_pool(i)
+            pick_var(i)
             scale_by_gain(nc.gpsimd, i)
-            if i in (1, 2):
-                round_w1(S_, 1, i - 1, 0, 0, 128)
-                quantize_w1(1, i - 1, 0, 4)
+        h_out(0, S_, V_)
+        round_w1(V_, 1, 0, 0, 0, 64)
+        picks(0)
+        h_out(1)
+        picks(1)
+        round_w1(S_, 1, 0, 256, 64, 128)
+        quantize_w1(1, 0, 0, 4)
+        h_out(2)
+        picks(2)
+        round_w1(S_, 1, 1, 0, 0, 128)
+        quantize_w1(1, 1, 0, 4)
+        h[3] = held([P, S], F32, "w1_raw11_0")
+        h_out(3)
+        picks(3)
         for i in range(4, 8):
             h_pass(i, 0)
             h_pass(i, 1)
+        square_ref_rest(0)
+        square_ref_rest(1)
         inv_root(0)
         inv_root(1)
+        square_ref_rest(2)
         square(0)
-        for i in range(4, 8):
-            h_out(i)
-            pick_ref(i)
-            square_ref_pool(i)
-            if i < 6:
-                pick_var(i)
-                scale_by_gain(nc.gpsimd, i)
-            if i == 4:
-                square(1)
+        square(1)
+        h_out(4)
+        picks(4)
+        square_ref_rest(3)
+        h_out(5)
+        picks(5)
+        square_ref_rest(4)
+        h_out(6)
+        pick_ref(6)
+        square_ref_pool(6)
+        h_out(7)
+        pick_ref(7)
+        square_ref_pool(7)
         inv_root(2)
         inv_root(3)
         pick_var(6)
         scale_by_gain(nc.gpsimd, 6)
         pick_var(7)
+        square_ref_rest(5)
         square(2)
         square(3)
         inv_root(4)
         inv_root(5)
+        square_ref_rest(6)
+        square_ref_rest(7)
         square(4)
         square(5)
         inv_root(6)
         inv_root(7)
         square(6)
         square(7)
-        scale_by_gain_scalar(7)
         make_z(0, 0)
+        scale_by_gain(nc.vector, 7)
         make_z(0, 1)
         quantize_z(0, 0)
         open_block(0, 0, 4, "bank")

@@ -60,9 +60,9 @@ def tile_list_variant_pathogenicity_score_kernel(
         def load_words(a):
             nc.sync.dma_start(tab_w[a][:], tab_words[a].rearrange("p t i -> p (t i)").bitcast(I32))
 
+        tab_s_words = tab_scales.bitcast(I32)
         nc.sync.dma_start(offs_sb[:], offs)
         load_words(0)
-        tab_s_words = tab_scales.bitcast(I32)
         for q in range(4):
             nc.sync.dma_start(tab_s[32 * q : 32 * q + 8, :], tab_s_words[:, 4 * q : 4 * q + 4, :])
         load_w1(0, 0, 0, 256)
@@ -73,9 +73,9 @@ def tile_list_variant_pathogenicity_score_kernel(
         load_w1(0, 1, 0, 256)
         load_w1(0, 1, 256, 512)
         load_w1(1, 0, 0, 256)
-        nc.sync.dma_start(gain_sb[:], gain.rearrange("(a p t) -> p a t", a=2, t=PACK))
         load_w1(1, 0, 256, 512)
         load_w1(1, 1, 0, 512)
+        nc.sync.dma_start(gain_sb[:], gain.rearrange("(a p t) -> p a t", a=2, t=PACK))
         nc.sync.dma_start(w4_w[:].bitcast(I32), w4_words.rearrange("a p c -> p a c").bitcast(I32))
         w4_s_words = w4_scales.bitcast(I32)
         for q in range(4):
@@ -99,20 +99,8 @@ def tile_list_variant_pathogenicity_score_kernel(
         w1_s = {}
         for g in range(2):
             for a in range(2):
-                if g == 0:
-                    w1_bf[g, a] = held([P, PACK, P, PACK], BF16, "w1_bf%d%d" % (g, a))
-                if (g, a) == (0, 1):
-                    w1_w[g, a] = held([P, 2 * P], U32, "w1_w01")
-                else:
-                    w1_w[g, a] = held([P, PASS], U32, "w1_w%d%d" % (g, a))
                 w1_s[g, a] = held([P, PASS], U8, "w1_s%d%d" % (g, a))
-
-        w1_w_last = held([P, 2 * P], U32, "w1_w_last")
-
-        def w1_codes(g, a, t0, t1):
-            if (g, a) == (0, 1) and t0 >= 2:
-                return w1_w_last[:, (t0 - 2) * P : (t1 - 2) * P].bitcast(FP8X4)
-            return w1_w[g, a][:, t0 * P : t1 * P].bitcast(FP8X4)
+                w1_w[g, a] = held([P, PASS], U32, "w1_w%d%d" % (g, a))
 
         def round_w1(copy, g, a, c0, m0, m1):
             src = w1_raw[g, a, c0][:].rearrange("p j (m t) -> p m j t", t=PACK)[:, m0 - c0 // PACK : m1 - c0 // PACK]
@@ -122,12 +110,12 @@ def tile_list_variant_pathogenicity_score_kernel(
         def quantize_w1(g, a, t0, t1):
             cols = slice(t0 * P, t1 * P)
             nc.vector.quantize_mx(
-                out=w1_codes(g, a, t0, t1),
+                out=w1_w[g, a][:, cols].bitcast(FP8X4),
                 scales=w1_s[g, a][:, cols],
                 in_=w1_bf[g, a][:, t0:t1].rearrange("p t m j -> p (t m j)"),
             )
 
-        h = {i: held([P, S], F32, "h%d" % i) for i in range(8) if i != 3}
+        h = {}
         h_bank = {}
 
         def h_pass(i, a):
@@ -138,7 +126,7 @@ def tile_list_variant_pathogenicity_score_kernel(
                     h_bank[i, u] = psum.tile([P, BANK], F32, name="bank")
                 nc.tensor.matmul_mx(
                     out=h_bank[i, u][:],
-                    lhsT=w1_codes(g, a, t, t + 1),
+                    lhsT=w1_w[g, a][:, cols].bitcast(FP8X4),
                     lhsT_scale=w1_s[g, a][:, cols],
                     rhs=v_w[a][:, hf].bitcast(FP8X4),
                     rhs_scale=v_s[4 * a : P, hf],
@@ -146,56 +134,42 @@ def tile_list_variant_pathogenicity_score_kernel(
                     stop=(a == 1),
                 )
 
-        def h_half(i, u):
-            nc.scalar.copy(h[i][:, halves[u]], h_bank[i, u][:])
+        S_, V_ = nc.scalar.copy, nc.vector.tensor_copy
 
-        def h_out(i, copy0=nc.scalar.copy, copy1=nc.scalar.copy):
+        def h_out(i, copy0=S_, copy1=S_, name=None):
+            h[i] = held([P, S], F32, name or "h%d" % i)
             copy0(h[i][:, halves[0]], h_bank[i, 0][:])
             copy1(h[i][:, halves[1]], h_bank[i, 1][:])
 
-        var = [held([P, PACK, NP], F32, "var%d" % g) for g in range(2)]
-        damp = [held([P, PACK, NP], F32, "damp%d" % g) for g in range(2)]
+        root = [held([P, NP], F32, "root%d" % i) for i in range(8)]
+        part = [held([P, PACK, NP], F32, "part%d" % g) for g in range(2)]
+        rest = [held([P, PACK, NP], F32, "rest%d" % g) for g in range(2)]
         z_w = [held([P, NP], U32, "z_w%d" % g) for g in range(2)]
         z_s = [held([P, NP], U8, "z_s%d" % g) for g in range(2)]
+        z_bf = {}
 
         def row(tiles, i):
             return tiles[i // PACK][:, i % PACK, :]
 
-        def ref(i):
-            return row(var, i + PACK) if i in (2, 3) else row(damp, i)
+        def gain_of(i):
+            g, t = divmod(i, PACK)
+            return gain_sb[:, g, t : t + 1]
 
         def pick_ref(i):
-            nc.vector.tensor_copy(ref(i), h[i][:].indirect(pos2_sb[:]))
+            nc.vector.tensor_copy(root[i][:], h[i][:].indirect(pos2_sb[:]))
+
+        def damp(i):
+            nc.scalar.activation(root[i][:], root[i][:], ACT.Square)
+            nc.scalar.activation(root[i][:], root[i][:], ACT.Abs_reciprocal_sqrt, bias=1.0)
 
         def pick_var(i):
-            nc.vector.tensor_copy(row(var, i), h[i][:].indirect(pos1_sb[:]))
+            nc.vector.tensor_tensor(row(part, i), h[i][:].indirect(pos1_sb[:]), root[i][:], MULT)
 
-        def square_ref(i):
-            nc.scalar.activation(ref(i), ref(i), ACT.Square)
+        def gain_s(i):
+            nc.scalar.activation(row(rest, i), root[i][:], ACT.Copy, scale=gain_of(i))
 
-        def square_ref_pool(i):
-            part = ref(i)[:, 0:SPLIT]
-            nc.gpsimd.tensor_tensor(part, part, part, MULT)
-
-        def square_ref_rest(i):
-            part = ref(i)[:, SPLIT:NP]
-            nc.scalar.activation(part, part, ACT.Square)
-
-        def inv_root(i):
-            nc.scalar.activation(row(damp, i), ref(i), ACT.Abs_reciprocal_sqrt, bias=1.0)
-
-        def scale_by_gain_scalar(i):
-            g, t = divmod(i, PACK)
-            nc.scalar.activation(row(var, i), row(var, i), ACT.Copy, scale=gain_sb[:, g, t : t + 1])
-
-        def square(i):
-            nc.scalar.activation(row(damp, i), row(damp, i), ACT.Square)
-
-        def scale_by_gain(engine, i):
-            g, t = divmod(i, PACK)
-            engine.tensor_scalar(row(var, i), row(var, i), gain_sb[:, g, t : t + 1], 0.0, MULT, ADD)
-
-        z_bf = {}
+        def gain_v(i):
+            nc.vector.tensor_scalar(row(rest, i), root[i][:], gain_of(i), 0.0, MULT, ADD)
 
         def make_z(g, b):
             cols = slice(b * P, (b + 1) * P)
@@ -203,8 +177,8 @@ def tile_list_variant_pathogenicity_score_kernel(
                 z_bf[b] = keep.tile([P, 2, P, PACK], BF16, name="z_bf", align_bytes=64, bufs=2)
             nc.vector.tensor_tensor(
                 z_bf[b][:, g].rearrange("p (c i) t -> p c t i", i=4),
-                var[g][:, :, cols].rearrange("p t (c i) -> p c t i", i=4),
-                damp[g][:, :, cols].rearrange("p t (c i) -> p c t i", i=4),
+                part[g][:, :, cols].rearrange("p t (c i) -> p c t i", i=4),
+                rest[g][:, :, cols].rearrange("p t (c i) -> p c t i", i=4),
                 MULT,
             )
 
@@ -233,8 +207,8 @@ def tile_list_variant_pathogenicity_score_kernel(
         res = held([P, PACK, PACK, P], F32, "res")
         y_bank = {}
 
-        def open_block(b, n0, n1, tag):
-            y_bank[b, n0] = psum.tile([P, n1 - n0, P], F32, name=tag)
+        def open_block(b, n0, n1):
+            y_bank[b, n0] = psum.tile([P, n1 - n0, P], F32, name="bank")
             for nt in range(n0, n1):
                 y_pass(y_bank[b, n0][:, nt - n0, :], nt, 0, slice(b * P, (b + 1) * P), nt == n0, False)
 
@@ -245,9 +219,9 @@ def tile_list_variant_pathogenicity_score_kernel(
             nc.scalar.activation(res[:, b, n0:n1], y_bank[b, n0][:], ACT.Sigmoid)
             nc.sync.dma_start(out_v[:, n0:n1, cols], res[:, b, n0:n1])
 
-        SPLIT = 256
-        S_, V_ = nc.scalar.copy, nc.vector.tensor_copy
-
+        for g in range(2):
+            for a in range(2):
+                w1_bf[g, a] = held([P, PACK, P, PACK], BF16, "w1_bf%d%d" % (g, a))
         pick_words(0)
         pick_scales()
         round_w1(S_, 0, 0, 0, 0, 64)
@@ -264,74 +238,55 @@ def tile_list_variant_pathogenicity_score_kernel(
             h_pass(i, 0)
             h_pass(i, 1)
 
-        w1_bf[1, 0] = held([P, PACK, P, PACK], BF16, "w1_w01")
-        w1_bf[1, 1] = held([P, PACK, P, PACK], BF16, "w1_w_last")
-        def picks(i):
-            pick_ref(i)
-            square_ref_pool(i)
+        def square(i):
+            nc.scalar.activation(root[i][:], root[i][:], ACT.Square)
+
+        def inv_root(i):
+            nc.scalar.activation(root[i][:], root[i][:], ACT.Abs_reciprocal_sqrt, bias=1.0)
+
+        def damp_pair(i):
+            square(i)
+            square(i + 1)
+            inv_root(i)
+            inv_root(i + 1)
             pick_var(i)
-            scale_by_gain(nc.gpsimd, i)
-        h_out(0, S_, V_)
+            pick_var(i + 1)
+
         round_w1(V_, 1, 0, 0, 0, 64)
-        picks(0)
-        h_out(1)
-        picks(1)
-        round_w1(S_, 1, 0, 256, 64, 128)
+        h_out(0, S_, V_)
+        round_w1(V_, 1, 0, 256, 64, 128)
+        pick_ref(0)
         quantize_w1(1, 0, 0, 4)
-        h_out(2)
-        picks(2)
-        round_w1(S_, 1, 1, 0, 0, 128)
+        for i in range(1, 4):
+            h_out(i)
+            pick_ref(i)
+        round_w1(V_, 1, 1, 0, 0, 36)
+        round_w1(S_, 1, 1, 0, 36, 128)
         quantize_w1(1, 1, 0, 4)
-        h[3] = held([P, S], F32, "w1_raw11_0")
-        h_out(3)
-        picks(3)
         for i in range(4, 8):
             h_pass(i, 0)
             h_pass(i, 1)
-        square_ref_rest(0)
-        square_ref_rest(1)
-        inv_root(0)
-        inv_root(1)
-        square_ref_rest(2)
-        square(0)
-        square(1)
-        h_out(4)
-        picks(4)
-        square_ref_rest(3)
-        h_out(5)
-        picks(5)
-        square_ref_rest(4)
-        h_out(6)
-        pick_ref(6)
-        square_ref_pool(6)
-        h_out(7)
-        pick_ref(7)
-        square_ref_pool(7)
-        inv_root(2)
-        inv_root(3)
-        pick_var(6)
-        scale_by_gain(nc.gpsimd, 6)
-        pick_var(7)
-        square_ref_rest(5)
-        square(2)
-        square(3)
-        inv_root(4)
-        inv_root(5)
-        square_ref_rest(6)
-        square_ref_rest(7)
-        square(4)
-        square(5)
-        inv_root(6)
-        inv_root(7)
-        square(6)
-        square(7)
+        damp_pair(0)
+        damp_pair(2)
+        for i in (4, 5):
+            h_out(i)
+            pick_ref(i)
+        for i in range(4):
+            gain_s(i)
         make_z(0, 0)
-        scale_by_gain(nc.vector, 7)
         make_z(0, 1)
         quantize_z(0, 0)
-        open_block(0, 0, 4, "bank")
         quantize_z(0, 1)
-        open_block(1, 0, 4, "bank")
+        for i in (6, 7):
+            h_out(i)
+            pick_ref(i)
+        open_block(0, 0, 4)
+        open_block(1, 0, 4)
+        damp_pair(4)
+        damp_pair(6)
+        for i in range(4, 8):
+            gain_s(i)
+
         make_z(1, 0)
         make_z(1, 1)
         quantize_z(1, 0)
@@ -341,14 +296,14 @@ def tile_list_variant_pathogenicity_score_kernel(
         close_block(1, 0, 4)
         make_z(1, 2)
         quantize_z(0, 2)
-        open_block(2, 0, 4, "bank")
+        open_block(2, 0, 4)
         make_z(0, 3)
         quantize_z(1, 2)
         close_block(2, 0, 4)
-        quantize_z(0, 3)
-        open_block(3, 0, 2, "bank")
-        open_block(3, 2, 4, "bank")
         make_z(1, 3)
+        quantize_z(0, 3)
+        open_block(3, 0, 2)
+        open_block(3, 2, 4)
         quantize_z(1, 3)
         close_block(3, 0, 2)
         close_block(3, 2, 4)

@@ -97,14 +97,33 @@ def tile_list_variant_pathogenicity_score_kernel(
         w1_bf = {}
         w1_w = {}
         w1_s = {}
-        for g in range(2):
+        w1_bf_g, w1_w_g, w1_s_g = {}, {}, {}
+        for a in range(2):
+            w1_bf[0, a] = held([P, PACK, P, PACK], BF16, "w1_bf0%d" % a)[:]
+            w1_w[0, a] = held([P, PASS], U32, "w1_w0%d" % a)[:]
+            w1_s[0, a] = held([P, PASS], U8, "w1_s0%d" % a)[:]
+        for g in (1,):
+            w1_bf_g[g] = held([P, 2, PACK, P, PACK], BF16, "w1_bf%d" % g)
+            w1_w_g[g] = held([P, 2, PASS], U32, "w1_w%d" % g)
+            w1_s_g[g] = held([P, 2, PASS], U8, "w1_s%d" % g)
             for a in range(2):
-                w1_s[g, a] = held([P, PASS], U8, "w1_s%d%d" % (g, a))
-                w1_w[g, a] = held([P, PASS], U32, "w1_w%d%d" % (g, a))
+                w1_bf[g, a] = w1_bf_g[g][:, a]
+                w1_w[g, a] = w1_w_g[g][:, a]
+                w1_s[g, a] = w1_s_g[g][:, a]
+
+        def pool_copy(dst, src):
+            nc.gpsimd.tensor_scalar(dst.rearrange("p m j t -> p t m j"), src.rearrange("p m j t -> p t m j"), 1.0, 0.0, MULT, ADD)
+
+        def quantize_group(g):
+            nc.vector.quantize_mx(
+                out=w1_w_g[g][:].rearrange("p a c -> p (a c)").bitcast(FP8X4),
+                scales=w1_s_g[g][:].rearrange("p a c -> p (a c)"),
+                in_=w1_bf_g[g][:].rearrange("p a t m j -> p (a t m j)"),
+            )
 
         def round_w1(copy, g, a, c0, m0, m1):
             src = w1_raw[g, a, c0][:].rearrange("p j (m t) -> p m j t", t=PACK)[:, m0 - c0 // PACK : m1 - c0 // PACK]
-            dst = w1_bf[g, a][:].rearrange("p t m j -> p m j t")[:, m0:m1]
+            dst = w1_bf[g, a].rearrange("p t m j -> p m j t")[:, m0:m1]
             copy(dst, src)
 
         def quantize_w1(g, a, t0, t1):
@@ -118,21 +137,24 @@ def tile_list_variant_pathogenicity_score_kernel(
         h = {}
         h_bank = {}
 
-        def h_pass(i, a):
+        def h_one(i, a, u):
             g, t = divmod(i, PACK)
             cols = slice(t * P, (t + 1) * P)
-            for u, hf in enumerate(halves):
-                if a == 0:
-                    h_bank[i, u] = psum.tile([P, BANK], F32, name="bank")
-                nc.tensor.matmul_mx(
-                    out=h_bank[i, u][:],
-                    lhsT=w1_w[g, a][:, cols].bitcast(FP8X4),
-                    lhsT_scale=w1_s[g, a][:, cols],
-                    rhs=v_w[a][:, hf].bitcast(FP8X4),
-                    rhs_scale=v_s[4 * a : P, hf],
-                    start=(a == 0),
-                    stop=(a == 1),
-                )
+            if a == 0:
+                h_bank[i, u] = psum.tile([P, BANK], F32, name="bank")
+            nc.tensor.matmul_mx(
+                out=h_bank[i, u][:],
+                lhsT=w1_w[g, a][:, cols].bitcast(FP8X4),
+                lhsT_scale=w1_s[g, a][:, cols],
+                rhs=v_w[a][:, halves[u]].bitcast(FP8X4),
+                rhs_scale=v_s[4 * a : P, halves[u]],
+                start=(a == 0),
+                stop=(a == 1),
+            )
+
+        def h_pass(i, a):
+            for u in range(2):
+                h_one(i, a, u)
 
         S_, V_ = nc.scalar.copy, nc.vector.tensor_copy
 
@@ -143,7 +165,7 @@ def tile_list_variant_pathogenicity_score_kernel(
 
         root = [held([P, NP], F32, "root%d" % i) for i in range(8)]
         part = [held([P, PACK, NP], F32, "part%d" % g) for g in range(2)]
-        rest = [held([P, PACK, NP], F32, "rest%d" % g) for g in range(2)]
+        rest = {1: held([P, PACK, NP], F32, "rest1")}
         z_w = [held([P, NP], U32, "z_w%d" % g) for g in range(2)]
         z_s = [held([P, NP], U8, "z_s%d" % g) for g in range(2)]
         z_bf = {}
@@ -167,6 +189,14 @@ def tile_list_variant_pathogenicity_score_kernel(
 
         def gain_s(i):
             nc.scalar.activation(row(rest, i), root[i][:], ACT.Copy, scale=gain_of(i))
+
+        def gain_g(i):
+            nc.gpsimd.tensor_scalar(row(rest, i), root[i][:], gain_of(i), 0.0, MULT, ADD)
+
+        def h_tile(i):
+            for u in range(2):
+                for a in range(2):
+                    h_one(i, a, u)
 
         def gain_v(i):
             nc.vector.tensor_scalar(row(rest, i), root[i][:], gain_of(i), 0.0, MULT, ADD)
@@ -219,9 +249,6 @@ def tile_list_variant_pathogenicity_score_kernel(
             nc.scalar.activation(res[:, b, n0:n1], y_bank[b, n0][:], ACT.Sigmoid)
             nc.sync.dma_start(out_v[:, n0:n1, cols], res[:, b, n0:n1])
 
-        for g in range(2):
-            for a in range(2):
-                w1_bf[g, a] = held([P, PACK, P, PACK], BF16, "w1_bf%d%d" % (g, a))
         pick_words(0)
         pick_scales()
         round_w1(S_, 0, 0, 0, 0, 64)
@@ -254,32 +281,29 @@ def tile_list_variant_pathogenicity_score_kernel(
 
         round_w1(V_, 1, 0, 0, 0, 64)
         h_out(0, S_, V_)
-        round_w1(V_, 1, 0, 256, 64, 128)
+        round_w1(pool_copy, 1, 0, 256, 64, 128)
         pick_ref(0)
-        quantize_w1(1, 0, 0, 4)
         for i in range(1, 4):
             h_out(i)
             pick_ref(i)
-        round_w1(V_, 1, 1, 0, 0, 36)
-        round_w1(S_, 1, 1, 0, 36, 128)
-        quantize_w1(1, 1, 0, 4)
+        round_w1(pool_copy, 1, 1, 0, 60, 128)
+        round_w1(S_, 1, 1, 0, 0, 60)
+        quantize_group(1)
         for i in range(4, 8):
-            h_pass(i, 0)
-            h_pass(i, 1)
+            h_tile(i)
         damp_pair(0)
         damp_pair(2)
-        for i in (4, 5):
+        rest[0] = held([P, PACK, NP], F32, "h3")
+        for i in range(3):
+            gain_g(i)
+        for i in range(4, 8):
             h_out(i)
             pick_ref(i)
-        for i in range(4):
-            gain_s(i)
+        gain_s(3)
         make_z(0, 0)
         make_z(0, 1)
         quantize_z(0, 0)
         quantize_z(0, 1)
-        for i in (6, 7):
-            h_out(i)
-            pick_ref(i)
         open_block(0, 0, 4)
         open_block(1, 0, 4)
         damp_pair(4)

@@ -45,7 +45,7 @@ def tile_list_variant_pathogenicity_score_kernel(
 
         one = held([P, 1], F32, "one")
         warm = held([P, 1], F32, "warm")
-        nc.vector.memset(tab_s[:], 0)
+        nc.gpsimd.memset(tab_s[:], 0)
         nc.vector.memset(one[:], 1.0)
         nc.scalar.activation(warm[:], one[:], ACT.Abs_reciprocal_sqrt)
         nc.gpsimd.memset(w4_s[:], 0)
@@ -61,13 +61,12 @@ def tile_list_variant_pathogenicity_score_kernel(
             nc.sync.dma_start(tab_w[a][:], tab_words[a].rearrange("p t i -> p (t i)").bitcast(I32))
 
         tab_s_words = tab_scales.bitcast(I32)
-        nc.sync.dma_start(offs_sb[:], offs)
         load_words(0)
+        nc.sync.dma_start(offs_sb[:], offs)
         for q in range(4):
             nc.sync.dma_start(tab_s[32 * q : 32 * q + 8, :], tab_s_words[:, 4 * q : 4 * q + 4, :])
-        load_w1(0, 0, 0, 256)
         nc.sync.dma_start(pos2_sb[:], pos2)
-        nc.sync.dma_start(pos1_sb[:], pos1)
+        load_w1(0, 0, 0, 256)
         load_w1(0, 0, 256, 512)
         load_words(1)
         load_w1(0, 1, 0, 256)
@@ -75,6 +74,7 @@ def tile_list_variant_pathogenicity_score_kernel(
         load_w1(1, 0, 0, 256)
         load_w1(1, 0, 256, 512)
         load_w1(1, 1, 0, 512)
+        nc.sync.dma_start(pos1_sb[:], pos1)
         nc.sync.dma_start(gain_sb[:], gain.rearrange("(a p t) -> p a t", a=2, t=PACK))
         nc.sync.dma_start(w4_w[:].bitcast(I32), w4_words.rearrange("a p c -> p a c").bitcast(I32))
         w4_s_words = w4_scales.bitcast(I32)
@@ -121,10 +121,10 @@ def tile_list_variant_pathogenicity_score_kernel(
                 in_=w1_bf_g[g][:].rearrange("p a t m j -> p (a t m j)"),
             )
 
-        def round_w1(copy, g, a, c0, m0, m1):
+        def round_w1(copy, g, a, c0, m0, m1, t0=0, t1=PACK):
             src = w1_raw[g, a, c0][:].rearrange("p j (m t) -> p m j t", t=PACK)[:, m0 - c0 // PACK : m1 - c0 // PACK]
             dst = w1_bf[g, a].rearrange("p t m j -> p m j t")[:, m0:m1]
-            copy(dst, src)
+            copy(dst[:, :, :, t0:t1], src[:, :, :, t0:t1])
 
         def quantize_w1(g, a, t0, t1):
             cols = slice(t0 * P, t1 * P)
@@ -253,11 +253,14 @@ def tile_list_variant_pathogenicity_score_kernel(
         pick_scales()
         round_w1(S_, 0, 0, 0, 0, 64)
         round_w1(S_, 0, 0, 256, 64, 128)
-        quantize_w1(0, 0, 0, 4)
+        quantize_w1(0, 0, 0, 1)
+        quantize_w1(0, 0, 1, 2)
+        quantize_w1(0, 0, 2, 4)
         pick_words(1)
-        round_w1(S_, 0, 1, 0, 0, 64)
-        round_w1(S_, 0, 1, 256, 64, 84)
-        round_w1(V_, 0, 1, 256, 84, 128)
+        round_w1(S_, 0, 1, 0, 0, 64, 0, 2)
+        round_w1(S_, 0, 1, 0, 0, 64, 2, 4)
+        round_w1(V_, 0, 1, 256, 64, 128, 0, 2)
+        round_w1(S_, 0, 1, 256, 64, 128, 2, 4)
         quantize_w1(0, 1, 0, 1)
         quantize_w1(0, 1, 1, 2)
         quantize_w1(0, 1, 2, 4)
@@ -271,13 +274,21 @@ def tile_list_variant_pathogenicity_score_kernel(
         def inv_root(i):
             nc.scalar.activation(root[i][:], root[i][:], ACT.Abs_reciprocal_sqrt, bias=1.0)
 
+        def pick_var_part(i, c0, c1):
+            picked = h[i][:].indirect(pos1_sb[:, c0 // 16 : c1 // 16])
+            nc.vector.tensor_tensor(row(part, i)[:, c0:c1], picked, root[i][:, c0:c1], MULT)
+
         def damp_pair(i):
             square(i)
             square(i + 1)
             inv_root(i)
             inv_root(i + 1)
             pick_var(i)
-            pick_var(i + 1)
+            if i + 1 < 7:
+                pick_var(i + 1)
+            else:
+                pick_var_part(7, 0, 256)
+                pick_var_part(7, 256, 512)
 
         round_w1(V_, 1, 0, 0, 0, 64)
         h_out(0, S_, V_)
@@ -286,8 +297,8 @@ def tile_list_variant_pathogenicity_score_kernel(
         for i in range(1, 4):
             h_out(i)
             pick_ref(i)
-        round_w1(pool_copy, 1, 1, 0, 60, 128)
-        round_w1(S_, 1, 1, 0, 0, 60)
+        round_w1(pool_copy, 1, 1, 0, 0, 128, 2, 4)
+        round_w1(S_, 1, 1, 0, 0, 128, 0, 2)
         quantize_group(1)
         for i in range(4, 8):
             h_tile(i)

@@ -163,7 +163,8 @@ def tile_list_variant_pathogenicity_score_kernel(
             copy0(h[i][:, halves[0]], h_bank[i, 0][:])
             copy1(h[i][:, halves[1]], h_bank[i, 1][:])
 
-        root = [held([P, NP], F32, "root%d" % i) for i in range(8)]
+        root0 = held([P, PACK, NP], F32, "root0")
+        root = [root0[:, i, :] for i in range(PACK)] + [held([P, NP], F32, "root%d" % i)[:] for i in range(PACK, 8)]
         part = [held([P, PACK, NP], F32, "part%d" % g) for g in range(2)]
         rest = {1: held([P, PACK, NP], F32, "rest1")}
         z_w = [held([P, NP], U32, "z_w%d" % g) for g in range(2)]
@@ -178,20 +179,20 @@ def tile_list_variant_pathogenicity_score_kernel(
             return gain_sb[:, g, t : t + 1]
 
         def pick_ref(i):
-            nc.vector.tensor_copy(root[i][:], h[i][:].indirect(pos2_sb[:]))
+            nc.vector.tensor_copy(root[i], h[i][:].indirect(pos2_sb[:]))
 
         def damp(i):
-            nc.scalar.activation(root[i][:], root[i][:], ACT.Square)
-            nc.scalar.activation(root[i][:], root[i][:], ACT.Abs_reciprocal_sqrt, bias=1.0)
+            nc.scalar.activation(root[i], root[i], ACT.Square)
+            nc.scalar.activation(root[i], root[i], ACT.Abs_reciprocal_sqrt, bias=1.0)
 
         def pick_var(i):
-            nc.vector.tensor_tensor(row(part, i), h[i][:].indirect(pos1_sb[:]), root[i][:], MULT)
+            nc.vector.tensor_tensor(row(part, i), h[i][:].indirect(pos1_sb[:]), root[i], MULT)
 
         def gain_s(i):
-            nc.scalar.activation(row(rest, i), root[i][:], ACT.Copy, scale=gain_of(i))
+            nc.scalar.activation(row(rest, i), root[i], ACT.Copy, scale=gain_of(i))
 
         def gain_g(i):
-            nc.gpsimd.tensor_scalar(row(rest, i), root[i][:], gain_of(i), 0.0, MULT, ADD)
+            nc.gpsimd.tensor_scalar(row(rest, i), root[i], gain_of(i), 0.0, MULT, ADD)
 
         def h_tile(i):
             for u in range(2):
@@ -199,17 +200,38 @@ def tile_list_variant_pathogenicity_score_kernel(
                     h_one(i, a, u)
 
         def gain_v(i):
-            nc.vector.tensor_scalar(row(rest, i), root[i][:], gain_of(i), 0.0, MULT, ADD)
+            nc.vector.tensor_scalar(row(rest, i), root[i], gain_of(i), 0.0, MULT, ADD)
 
         def make_z(g, b):
             cols = slice(b * P, (b + 1) * P)
-            if g == 0:
+            if g == (1 if b < 2 else 0):
                 z_bf[b] = keep.tile([P, 2, P, PACK], BF16, name="z_bf", align_bytes=64, bufs=2)
             nc.vector.tensor_tensor(
                 z_bf[b][:, g].rearrange("p (c i) t -> p c t i", i=4),
                 part[g][:, :, cols].rearrange("p t (c i) -> p c t i", i=4),
-                rest[g][:, :, cols].rearrange("p t (c i) -> p c t i", i=4),
+                (rest[1] if g else root0)[:, :, cols].rearrange("p t (c i) -> p c t i", i=4),
                 MULT,
+            )
+
+        z_first = held([P, 2 * P, PACK], BF16, "z_first")
+
+        def make_z_pool(b):
+            cols = slice(b * P, (b + 1) * P)
+            nc.gpsimd.tensor_tensor(
+                z_first[:, cols],
+                part[0][:, :, cols].rearrange("p t j -> p j t"),
+                root0[:, :, cols].rearrange("p t j -> p j t"),
+                MULT,
+            )
+
+        first = {}
+
+        def quantize_first():
+            first[0] = held([P, 2 * P], U32, "h4")
+            nc.vector.quantize_mx(
+                out=first[0][:].bitcast(FP8X4),
+                scales=z_s[0][:, 0 : 2 * P],
+                in_=z_first[:].rearrange("p j t -> p (j t)"),
             )
 
         def quantize_z(g, b):
@@ -227,7 +249,7 @@ def tile_list_variant_pathogenicity_score_kernel(
                 out=dst,
                 lhsT=w4_w[:, g, 2 * P * nt : 2 * P * (nt + 1)].bitcast(FP4X4),
                 lhsT_scale=w4_s8[:, g * N + P * nt : g * N + P * (nt + 1)],
-                rhs=z_w[g][:, cols].bitcast(FP8X4),
+                rhs=(first[0] if g == 0 and cols.start < 2 * P else z_w[g])[:, cols].bitcast(FP8X4),
                 rhs_scale=z_s[g][:, cols],
                 start=start,
                 stop=stop,
@@ -269,10 +291,10 @@ def tile_list_variant_pathogenicity_score_kernel(
             h_pass(i, 1)
 
         def square(i):
-            nc.scalar.activation(root[i][:], root[i][:], ACT.Square)
+            nc.scalar.activation(root[i], root[i], ACT.Square)
 
         def inv_root(i):
-            nc.scalar.activation(root[i][:], root[i][:], ACT.Abs_reciprocal_sqrt, bias=1.0)
+            nc.scalar.activation(root[i], root[i], ACT.Abs_reciprocal_sqrt, bias=1.0)
 
         def pick_var_part(i, c0, c1):
             picked = h[i][:].indirect(pos1_sb[:, c0 // 16 : c1 // 16])
@@ -304,23 +326,24 @@ def tile_list_variant_pathogenicity_score_kernel(
             h_tile(i)
         damp_pair(0)
         damp_pair(2)
-        rest[0] = held([P, PACK, NP], F32, "h3")
-        for i in range(3):
-            gain_g(i)
+        for i in range(2):
+            nc.scalar.activation(row(part, i)[:, 0:256], row(part, i)[:, 0:256], ACT.Copy, scale=gain_of(i))
+        for i in range(2, 4):
+            nc.gpsimd.tensor_scalar(row(part, i)[:, 0:256], row(part, i)[:, 0:256], gain_of(i), 0.0, MULT, ADD)
+        make_z_pool(0)
+        make_z_pool(1)
         for i in range(4, 8):
             h_out(i)
             pick_ref(i)
-        gain_s(3)
-        make_z(0, 0)
-        make_z(0, 1)
-        quantize_z(0, 0)
-        quantize_z(0, 1)
+        damp_pair(4)
+        quantize_first()
         open_block(0, 0, 4)
         open_block(1, 0, 4)
-        damp_pair(4)
         damp_pair(6)
         for i in range(4, 8):
             gain_s(i)
+        for i in range(4):
+            nc.scalar.activation(row(part, i)[:, 256:NP], row(part, i)[:, 256:NP], ACT.Copy, scale=gain_of(i))
 
         make_z(1, 0)
         make_z(1, 1)

@@ -218,9 +218,9 @@ def tile_list_variant_pathogenicity_score_kernel(
         def make_z_pool(b):
             cols = slice(b * P, (b + 1) * P)
             nc.gpsimd.tensor_tensor(
-                z_first[:, cols],
-                part[0][:, :, cols].rearrange("p t j -> p j t"),
-                root0[:, :, cols].rearrange("p t j -> p j t"),
+                z_first[:, cols].rearrange("p (c i) t -> p c t i", i=4),
+                part[0][:, :, cols].rearrange("p t (c i) -> p c t i", i=4),
+                root0[:, :, cols].rearrange("p t (c i) -> p c t i", i=4),
                 MULT,
             )
 

@@ -112,7 +112,7 @@ def tile_list_variant_pathogenicity_score_kernel(
                 w1_s[g, a] = w1_s_g[g][:, a]
 
         def pool_copy(dst, src):
-            nc.gpsimd.tensor_scalar(dst.rearrange("p m j t -> p t m j"), src.rearrange("p m j t -> p t m j"), 1.0, 0.0, MULT, ADD)
+            nc.gpsimd.tensor_scalar(dst.rearrange("p m j t -> p m t j"), src.rearrange("p m j t -> p m t j"), 1.0, 0.0, MULT, ADD)
 
         def quantize_group(g):
             nc.vector.quantize_mx(
@@ -163,10 +163,9 @@ def tile_list_variant_pathogenicity_score_kernel(
             copy0(h[i][:, halves[0]], h_bank[i, 0][:])
             copy1(h[i][:, halves[1]], h_bank[i, 1][:])
 
-        root0 = held([P, PACK, NP], F32, "root0")
-        root = [root0[:, i, :] for i in range(PACK)] + [held([P, NP], F32, "root%d" % i)[:] for i in range(PACK, 8)]
+        root = [held([P, NP], F32, "root%d" % i)[:] for i in range(8)]
         part = [held([P, PACK, NP], F32, "part%d" % g) for g in range(2)]
-        rest = {1: held([P, PACK, NP], F32, "rest1")}
+        rest = [held([P, PACK, NP], F32, "rest%d" % g) for g in range(2)]
         z_w = [held([P, NP], U32, "z_w%d" % g) for g in range(2)]
         z_s = [held([P, NP], U8, "z_s%d" % g) for g in range(2)]
         z_bf = {}
@@ -209,7 +208,7 @@ def tile_list_variant_pathogenicity_score_kernel(
             nc.vector.tensor_tensor(
                 z_bf[b][:, g].rearrange("p (c i) t -> p c t i", i=4),
                 part[g][:, :, cols].rearrange("p t (c i) -> p c t i", i=4),
-                (rest[1] if g else root0)[:, :, cols].rearrange("p t (c i) -> p c t i", i=4),
+                rest[g][:, :, cols].rearrange("p t (c i) -> p c t i", i=4),
                 MULT,
             )
 
@@ -220,7 +219,7 @@ def tile_list_variant_pathogenicity_score_kernel(
             nc.gpsimd.tensor_tensor(
                 z_first[:, cols].rearrange("p (c i) t -> p c t i", i=4),
                 part[0][:, :, cols].rearrange("p t (c i) -> p c t i", i=4),
-                root0[:, :, cols].rearrange("p t (c i) -> p c t i", i=4),
+                rest[0][:, :, cols].rearrange("p t (c i) -> p c t i", i=4),
                 MULT,
             )
 
@@ -319,20 +318,21 @@ def tile_list_variant_pathogenicity_score_kernel(
         for i in range(1, 4):
             h_out(i)
             pick_ref(i)
+        round_w1(pool_copy, 1, 1, 0, 96, 128, 0, 2)
         round_w1(pool_copy, 1, 1, 0, 0, 128, 2, 4)
-        round_w1(S_, 1, 1, 0, 0, 128, 0, 2)
+        round_w1(S_, 1, 1, 0, 0, 96, 0, 2)
         quantize_group(1)
         for i in range(4, 8):
             h_tile(i)
         damp_pair(0)
         damp_pair(2)
-        for i in range(2):
-            nc.scalar.activation(row(part, i)[:, 0:256], row(part, i)[:, 0:256], ACT.Copy, scale=gain_of(i))
-        for i in range(2, 4):
-            nc.gpsimd.tensor_scalar(row(part, i)[:, 0:256], row(part, i)[:, 0:256], gain_of(i), 0.0, MULT, ADD)
+        for i in range(4):
+            nc.scalar.activation(row(rest, i)[:, 0:256], root[i][:, 0:256], ACT.Copy, scale=gain_of(i))
+        h_out(4)
+        pick_ref(4)
         make_z_pool(0)
         make_z_pool(1)
-        for i in range(4, 8):
+        for i in range(5, 8):
             h_out(i)
             pick_ref(i)
         damp_pair(4)
@@ -343,7 +343,7 @@ def tile_list_variant_pathogenicity_score_kernel(
         for i in range(4, 8):
             gain_s(i)
         for i in range(4):
-            nc.scalar.activation(row(part, i)[:, 256:NP], row(part, i)[:, 256:NP], ACT.Copy, scale=gain_of(i))
+            nc.scalar.activation(row(rest, i)[:, 256:NP], root[i][:, 256:NP], ACT.Copy, scale=gain_of(i))
 
         make_z(1, 0)
         make_z(1, 1)

@@ -21,6 +21,8 @@ P = 128
 PACK = 4
 PASS = P * PACK
 BANK = 512
+HALF = 256
+TILES = H // P
 
 
 def tile_list_variant_pathogenicity_score_kernel(
@@ -43,9 +45,9 @@ def tile_list_variant_pathogenicity_score_kernel(
         w4_w = held([P, 2, 2 * N], U8, "w4_w")
         gain_sb = held([P, 2, PACK], F32, "gain_sb")
 
+        nc.gpsimd.memset(tab_s[:], 0)
         one = held([P, 1], F32, "one")
         warm = held([P, 1], F32, "warm")
-        nc.gpsimd.memset(tab_s[:], 0)
         nc.vector.memset(one[:], 1.0)
         nc.scalar.activation(warm[:], one[:], ACT.Abs_reciprocal_sqrt)
         nc.gpsimd.memset(w4_s[:], 0)
@@ -60,308 +62,259 @@ def tile_list_variant_pathogenicity_score_kernel(
         def load_words(a):
             nc.sync.dma_start(tab_w[a][:], tab_words[a].rearrange("p t i -> p (t i)").bitcast(I32))
 
-        tab_s_words = tab_scales.bitcast(I32)
         load_words(0)
         nc.sync.dma_start(offs_sb[:], offs)
+        tab_s_words = tab_scales.bitcast(I32)
         for q in range(4):
             nc.sync.dma_start(tab_s[32 * q : 32 * q + 8, :], tab_s_words[:, 4 * q : 4 * q + 4, :])
         nc.sync.dma_start(pos2_sb[:], pos2)
-        load_w1(0, 0, 0, 256)
-        load_w1(0, 0, 256, 512)
+        load_w1(0, 0, 0, HALF)
+        load_w1(0, 0, HALF, PASS)
         load_words(1)
-        load_w1(0, 1, 0, 256)
-        load_w1(0, 1, 256, 512)
-        load_w1(1, 0, 0, 256)
-        load_w1(1, 0, 256, 512)
-        load_w1(1, 1, 0, 512)
+        load_w1(0, 1, 0, HALF)
+        load_w1(0, 1, HALF, PASS)
+        load_w1(1, 0, 0, HALF)
+        load_w1(1, 0, HALF, PASS)
+        load_w1(1, 1, 0, PASS)
         nc.sync.dma_start(pos1_sb[:], pos1)
-        nc.sync.dma_start(gain_sb[:], gain.rearrange("(a p t) -> p a t", a=2, t=PACK))
-        nc.sync.dma_start(w4_w[:].bitcast(I32), w4_words.rearrange("a p c -> p a c").bitcast(I32))
+        nc.sync.dma_start(gain_sb[:], gain.rearrange("(g p t) -> p g t", g=2, t=PACK))
+        nc.sync.dma_start(w4_w[:].bitcast(I32), w4_words.rearrange("g p c -> p g c").bitcast(I32))
         w4_s_words = w4_scales.bitcast(I32)
         for q in range(4):
             nc.sync.dma_start(
-                w4_s[32 * q : 32 * q + 4, :].rearrange("r (a c) -> r a c", a=2),
-                w4_s_words[:, 4 * q : 4 * q + 4, :].rearrange("a r c -> r a c"),
+                w4_s[32 * q : 32 * q + 4, :].rearrange("r (g c) -> r g c", g=2),
+                w4_s_words[:, 4 * q : 4 * q + 4, :].rearrange("g r c -> r g c"),
             )
 
         v_s = held([P, S], U8, "v_s")
         v_w = [held([P, S], U32, "v_w%d" % a) for a in range(2)]
-        halves = [slice(0, BANK), slice(BANK, 2 * BANK)]
 
         def pick_words(a):
             nc.vector.tensor_copy(v_w[a][:], tab_w[a][:].bitcast(U32).indirect(offs_sb[:]))
 
-        def pick_scales():
-            nc.vector.tensor_copy(v_s[:], tab_s[:].bitcast(U8).indirect(offs_sb[:]))
-
-        w1_bf = {}
-        w1_w = {}
-        w1_s = {}
-        w1_bf_g, w1_w_g, w1_s_g = {}, {}, {}
+        w1_bf, w1_w, w1_s = {}, {}, {}
         for a in range(2):
             w1_bf[0, a] = held([P, PACK, P, PACK], BF16, "w1_bf0%d" % a)[:]
             w1_w[0, a] = held([P, PASS], U32, "w1_w0%d" % a)[:]
             w1_s[0, a] = held([P, PASS], U8, "w1_s0%d" % a)[:]
-        for g in (1,):
-            w1_bf_g[g] = held([P, 2, PACK, P, PACK], BF16, "w1_bf%d" % g)
-            w1_w_g[g] = held([P, 2, PASS], U32, "w1_w%d" % g)
-            w1_s_g[g] = held([P, 2, PASS], U8, "w1_s%d" % g)
-            for a in range(2):
-                w1_bf[g, a] = w1_bf_g[g][:, a]
-                w1_w[g, a] = w1_w_g[g][:, a]
-                w1_s[g, a] = w1_s_g[g][:, a]
+        w1_w_late = held([P, 2, PASS], U32, "w1_w1")
+        w1_s_late = held([P, 2, PASS], U8, "w1_s1")
+        for a in range(2):
+            w1_w[1, a] = w1_w_late[:, a]
+            w1_s[1, a] = w1_s_late[:, a]
 
-        def pool_copy(dst, src):
-            nc.gpsimd.tensor_scalar(dst.rearrange("p m j t -> p m t j"), src.rearrange("p m j t -> p m t j"), 1.0, 0.0, MULT, ADD)
-
-        def quantize_group(g):
-            nc.vector.quantize_mx(
-                out=w1_w_g[g][:].rearrange("p a c -> p (a c)").bitcast(FP8X4),
-                scales=w1_s_g[g][:].rearrange("p a c -> p (a c)"),
-                in_=w1_bf_g[g][:].rearrange("p a t m j -> p (a t m j)"),
-            )
-
-        def round_w1(copy, g, a, c0, m0, m1, t0=0, t1=PACK):
-            src = w1_raw[g, a, c0][:].rearrange("p j (m t) -> p m j t", t=PACK)[:, m0 - c0 // PACK : m1 - c0 // PACK]
-            dst = w1_bf[g, a].rearrange("p t m j -> p m j t")[:, m0:m1]
+        def round_w1(copy, g, a, c0, t0=0, t1=PACK):
+            src = w1_raw[g, a, c0][:].rearrange("p j (m t) -> p m j t", t=PACK)
+            m0 = c0 // PACK
+            dst = w1_bf[g, a].rearrange("p t m j -> p m j t")[:, m0 : m0 + src.shape[1]]
             copy(dst[:, :, :, t0:t1], src[:, :, :, t0:t1])
 
-        def quantize_w1(g, a, t0, t1):
+        def pool_round(dst, src):
+            order = "p m j t -> p m t j"
+            nc.gpsimd.tensor_scalar(dst.rearrange(order), src.rearrange(order), 1.0, 0.0, MULT, ADD)
+
+        def quantize_w1(a, t0, t1):
             cols = slice(t0 * P, t1 * P)
             nc.vector.quantize_mx(
-                out=w1_w[g, a][:, cols].bitcast(FP8X4),
-                scales=w1_s[g, a][:, cols],
-                in_=w1_bf[g, a][:, t0:t1].rearrange("p t m j -> p (t m j)"),
+                out=w1_w[0, a][:, cols].bitcast(FP8X4),
+                scales=w1_s[0, a][:, cols],
+                in_=w1_bf[0, a][:, t0:t1].rearrange("p t m j -> p (t m j)"),
             )
 
         h = {}
         h_bank = {}
 
-        def h_one(i, a, u):
+        def h_pass(i, a, u, width=BANK):
             g, t = divmod(i, PACK)
             cols = slice(t * P, (t + 1) * P)
+            entries = slice(u * width, (u + 1) * width)
             if a == 0:
-                h_bank[i, u] = psum.tile([P, BANK], F32, name="bank")
+                h_bank[i, u] = psum.tile([P, width], F32, name="bank")
             nc.tensor.matmul_mx(
                 out=h_bank[i, u][:],
                 lhsT=w1_w[g, a][:, cols].bitcast(FP8X4),
                 lhsT_scale=w1_s[g, a][:, cols],
-                rhs=v_w[a][:, halves[u]].bitcast(FP8X4),
-                rhs_scale=v_s[4 * a : P, halves[u]],
+                rhs=v_w[a][:, entries].bitcast(FP8X4),
+                rhs_scale=v_s[4 * a : P, entries],
                 start=(a == 0),
                 stop=(a == 1),
             )
 
-        def h_pass(i, a):
-            for u in range(2):
-                h_one(i, a, u)
-
-        S_, V_ = nc.scalar.copy, nc.vector.tensor_copy
-
-        def h_out(i, copy0=S_, copy1=S_, name=None):
-            h[i] = held([P, S], F32, name or "h%d" % i)
-            copy0(h[i][:, halves[0]], h_bank[i, 0][:])
-            copy1(h[i][:, halves[1]], h_bank[i, 1][:])
-
-        root = [held([P, NP], F32, "root%d" % i)[:] for i in range(8)]
-        part = [held([P, PACK, NP], F32, "part%d" % g) for g in range(2)]
-        rest = [held([P, PACK, NP], F32, "rest%d" % g) for g in range(2)]
-        z_w = [held([P, NP], U32, "z_w%d" % g) for g in range(2)]
-        z_s = [held([P, NP], U8, "z_s%d" % g) for g in range(2)]
-        z_bf = {}
-
-        def row(tiles, i):
-            return tiles[i // PACK][:, i % PACK, :]
-
-        def gain_of(i):
-            g, t = divmod(i, PACK)
-            return gain_sb[:, g, t : t + 1]
-
-        def pick_ref(i):
-            nc.vector.tensor_copy(root[i], h[i][:].indirect(pos2_sb[:]))
-
-        def damp(i):
-            nc.scalar.activation(root[i], root[i], ACT.Square)
-            nc.scalar.activation(root[i], root[i], ACT.Abs_reciprocal_sqrt, bias=1.0)
-
-        def pick_var(i):
-            nc.vector.tensor_tensor(row(part, i), h[i][:].indirect(pos1_sb[:]), root[i], MULT)
-
-        def gain_s(i):
-            nc.scalar.activation(row(rest, i), root[i], ACT.Copy, scale=gain_of(i))
-
-        def gain_g(i):
-            nc.gpsimd.tensor_scalar(row(rest, i), root[i], gain_of(i), 0.0, MULT, ADD)
-
         def h_tile(i):
             for u in range(2):
                 for a in range(2):
-                    h_one(i, a, u)
+                    h_pass(i, a, u)
 
-        def gain_v(i):
-            nc.vector.tensor_scalar(row(rest, i), root[i], gain_of(i), 0.0, MULT, ADD)
+        def h_out(i, copies=(nc.scalar.copy, nc.scalar.copy)):
+            h[i] = held([P, S], F32, "h%d" % i)
+            width = S // len(copies)
+            for u, copy in enumerate(copies):
+                copy(h[i][:, u * width : (u + 1) * width], h_bank[i, u][:])
+
+        root = [held([P, NP], F32, "root%d" % i) for i in range(TILES)]
+        a_root = [held([P, PACK, NP], F32, "a_root%d" % g) for g in range(2)]
+        gain_root = [held([P, PACK, NP], F32, "gain_root%d" % g) for g in range(2)]
+
+        def pick_ref(i):
+            nc.vector.tensor_copy(root[i][:], h[i][:].indirect(pos2_sb[:]))
+
+        def pick_var(i, j0, j1):
+            picked = h[i][:].indirect(pos1_sb[:, j0 // 16 : j1 // 16])
+            nc.vector.tensor_tensor(a_root[i // PACK][:, i % PACK, j0:j1], picked, root[i][:, j0:j1], MULT)
+
+        def damp_pair(i):
+            for n in (i, i + 1):
+                nc.scalar.activation(root[n][:], root[n][:], ACT.Square)
+            for n in (i, i + 1):
+                nc.scalar.activation(root[n][:], root[n][:], ACT.Abs_reciprocal_sqrt, bias=1.0)
+            pick_var(i, 0, NP)
+            if i + 1 < TILES - 1:
+                pick_var(i + 1, 0, NP)
+            else:
+                pick_var(i + 1, 0, HALF)
+                pick_var(i + 1, HALF, NP)
+
+        def apply_gain(g, j0, j1):
+            for t in range(PACK):
+                scale = gain_sb[:, g, t : t + 1]
+                nc.scalar.activation(gain_root[g][:, t, j0:j1], root[PACK * g + t][:, j0:j1], ACT.Copy, scale=scale)
+
+        z_w = [held([P, NP], U32, "z_w%d" % g) for g in range(2)]
+        z_s = [held([P, NP], U8, "z_s%d" % g) for g in range(2)]
+        z_first = held([P, HALF, PACK], BF16, "z_first")
+        z_codes = {(g, b): z_w[g][:, b * P : (b + 1) * P] for g in range(2) for b in range(4) if g == 1 or b >= 2}
+        z_bf = {}
+
+        def z_product(engine, dst, g, b):
+            cols = slice(b * P, (b + 1) * P)
+            engine.tensor_tensor(
+                dst.rearrange("p (c e) t -> p c t e", e=4),
+                a_root[g][:, :, cols].rearrange("p t (c e) -> p c t e", e=4),
+                gain_root[g][:, :, cols].rearrange("p t (c e) -> p c t e", e=4),
+                MULT,
+            )
 
         def make_z(g, b):
-            cols = slice(b * P, (b + 1) * P)
-            if g == (1 if b < 2 else 0):
+            if b not in z_bf:
                 z_bf[b] = keep.tile([P, 2, P, PACK], BF16, name="z_bf", align_bytes=64, bufs=2)
-            nc.vector.tensor_tensor(
-                z_bf[b][:, g].rearrange("p (c i) t -> p c t i", i=4),
-                part[g][:, :, cols].rearrange("p t (c i) -> p c t i", i=4),
-                rest[g][:, :, cols].rearrange("p t (c i) -> p c t i", i=4),
-                MULT,
-            )
-
-        z_first = held([P, 2 * P, PACK], BF16, "z_first")
-
-        def make_z_pool(b):
-            cols = slice(b * P, (b + 1) * P)
-            nc.gpsimd.tensor_tensor(
-                z_first[:, cols].rearrange("p (c i) t -> p c t i", i=4),
-                part[0][:, :, cols].rearrange("p t (c i) -> p c t i", i=4),
-                rest[0][:, :, cols].rearrange("p t (c i) -> p c t i", i=4),
-                MULT,
-            )
-
-        first = {}
-
-        def quantize_first():
-            first[0] = held([P, 2 * P], U32, "h4")
-            nc.vector.quantize_mx(
-                out=first[0][:].bitcast(FP8X4),
-                scales=z_s[0][:, 0 : 2 * P],
-                in_=z_first[:].rearrange("p j t -> p (j t)"),
-            )
+            z_product(nc.vector, z_bf[b][:, g], g, b)
 
         def quantize_z(g, b):
-            cols = slice(b * P, (b + 1) * P)
             nc.vector.quantize_mx(
-                out=z_w[g][:, cols].bitcast(FP8X4),
-                scales=z_s[g][:, cols],
+                out=z_codes[g, b].bitcast(FP8X4),
+                scales=z_s[g][:, b * P : (b + 1) * P],
                 in_=z_bf[b][:, g].rearrange("p j t -> p (j t)"),
             )
 
         w4_s8 = w4_s[:].bitcast(U8)
-
-        def y_pass(dst, nt, g, cols, start, stop):
-            nc.tensor.matmul_mx(
-                out=dst,
-                lhsT=w4_w[:, g, 2 * P * nt : 2 * P * (nt + 1)].bitcast(FP4X4),
-                lhsT_scale=w4_s8[:, g * N + P * nt : g * N + P * (nt + 1)],
-                rhs=(first[0] if g == 0 and cols.start < 2 * P else z_w[g])[:, cols].bitcast(FP8X4),
-                rhs_scale=z_s[g][:, cols],
-                start=start,
-                stop=stop,
-            )
-
         out_v = out.rearrange("(nt p) j -> p nt j", p=P)
-        res = held([P, PACK, PACK, P], F32, "res")
         y_bank = {}
 
-        def open_block(b, n0, n1):
-            y_bank[b, n0] = psum.tile([P, n1 - n0, P], F32, name="bank")
-            for nt in range(n0, n1):
-                y_pass(y_bank[b, n0][:, nt - n0, :], nt, 0, slice(b * P, (b + 1) * P), nt == n0, False)
-
-        def close_block(b, n0, n1):
-            cols = slice(b * P, (b + 1) * P)
-            for nt in range(n0, n1):
-                y_pass(y_bank[b, n0][:, nt - n0, :], nt, 1, cols, False, nt == n1 - 1)
-            nc.scalar.activation(res[:, b, n0:n1], y_bank[b, n0][:], ACT.Sigmoid)
-            nc.sync.dma_start(out_v[:, n0:n1, cols], res[:, b, n0:n1])
+        def y_passes(g, n0, n1, b0, b1):
+            if g == 0:
+                y_bank[n0, b0] = psum.tile([P, n1 - n0, (b1 - b0) * P], F32, name="bank")
+            bank = y_bank[n0, b0]
+            for b in range(b0, b1):
+                for nt in range(n0, n1):
+                    nc.tensor.matmul_mx(
+                        out=bank[:, nt - n0, (b - b0) * P : (b - b0 + 1) * P],
+                        lhsT=w4_w[:, g, 2 * P * nt : 2 * P * (nt + 1)].bitcast(FP4X4),
+                        lhsT_scale=w4_s8[:, g * N + P * nt : g * N + P * (nt + 1)],
+                        rhs=z_codes[g, b].bitcast(FP8X4),
+                        rhs_scale=z_s[g][:, b * P : (b + 1) * P],
+                        start=(g == 0 and (b, nt) == (b0, n0)),
+                        stop=(g == 1 and (b, nt) == (b1 - 1, n1 - 1)),
+                    )
+            if g == 1:
+                res = held([P, n1 - n0, (b1 - b0) * P], F32, "res%d%d" % (n0, b0))
+                nc.scalar.activation(res[:], bank[:], ACT.Sigmoid)
+                nc.sync.dma_start(out_v[:, n0:n1, b0 * P : b1 * P], res[:])
 
         pick_words(0)
-        pick_scales()
-        round_w1(S_, 0, 0, 0, 0, 64)
-        round_w1(S_, 0, 0, 256, 64, 128)
-        quantize_w1(0, 0, 0, 1)
-        quantize_w1(0, 0, 1, 2)
-        quantize_w1(0, 0, 2, 4)
+        nc.vector.tensor_copy(v_s[:], tab_s[:].bitcast(U8).indirect(offs_sb[:]))
+        round_w1(nc.scalar.copy, 0, 0, 0)
+        round_w1(nc.scalar.copy, 0, 0, HALF)
+        first_tiles = ((0, 1), (1, 2), (2, PACK))
+        for t0, t1 in first_tiles:
+            quantize_w1(0, t0, t1)
         pick_words(1)
-        round_w1(S_, 0, 1, 0, 0, 64, 0, 2)
-        round_w1(S_, 0, 1, 0, 0, 64, 2, 4)
-        round_w1(V_, 0, 1, 256, 64, 128, 0, 2)
-        round_w1(S_, 0, 1, 256, 64, 128, 2, 4)
-        quantize_w1(0, 1, 0, 1)
-        quantize_w1(0, 1, 1, 2)
-        quantize_w1(0, 1, 2, 4)
-        for i in range(4):
-            h_pass(i, 0)
-            h_pass(i, 1)
+        round_w1(nc.scalar.copy, 0, 1, 0, 0, 2)
+        round_w1(nc.scalar.copy, 0, 1, 0, 2, PACK)
+        round_w1(nc.vector.tensor_copy, 0, 1, HALF, 0, 2)
+        round_w1(nc.scalar.copy, 0, 1, HALF, 2, PACK)
+        for t0, t1 in first_tiles:
+            quantize_w1(1, t0, t1)
+        for a in range(2):
+            for u in range(4):
+                h_pass(0, a, u, HALF)
+        for i in (1, 2):
+            for a in range(2):
+                for u in range(2):
+                    h_pass(i, a, u)
+        h_tile(3)
 
-        def square(i):
-            nc.scalar.activation(root[i], root[i], ACT.Square)
-
-        def inv_root(i):
-            nc.scalar.activation(root[i], root[i], ACT.Abs_reciprocal_sqrt, bias=1.0)
-
-        def pick_var_part(i, c0, c1):
-            picked = h[i][:].indirect(pos1_sb[:, c0 // 16 : c1 // 16])
-            nc.vector.tensor_tensor(row(part, i)[:, c0:c1], picked, root[i][:, c0:c1], MULT)
-
-        def damp_pair(i):
-            square(i)
-            square(i + 1)
-            inv_root(i)
-            inv_root(i + 1)
-            pick_var(i)
-            if i + 1 < 7:
-                pick_var(i + 1)
-            else:
-                pick_var_part(7, 0, 256)
-                pick_var_part(7, 256, 512)
-
-        round_w1(V_, 1, 0, 0, 0, 64)
-        h_out(0, S_, V_)
-        round_w1(pool_copy, 1, 0, 256, 64, 128)
+        w1_bf_late = held([P, 2, PACK, P, PACK], BF16, "w1_bf01")
+        for a in range(2):
+            w1_bf[1, a] = w1_bf_late[:, a]
+        round_w1(pool_round, 1, 0, 0)
+        h_out(0, (nc.scalar.copy, nc.vector.tensor_copy) * 2)
+        round_w1(pool_round, 1, 0, HALF)
         pick_ref(0)
-        for i in range(1, 4):
+        for i in range(1, PACK):
             h_out(i)
             pick_ref(i)
-        round_w1(pool_copy, 1, 1, 0, 96, 128, 0, 2)
-        round_w1(pool_copy, 1, 1, 0, 0, 128, 2, 4)
-        round_w1(S_, 1, 1, 0, 0, 96, 0, 2)
-        quantize_group(1)
-        for i in range(4, 8):
+        round_w1(pool_round, 1, 1, 0, 2, PACK)
+        round_w1(nc.scalar.copy, 1, 1, 0, 0, 2)
+        nc.vector.quantize_mx(
+            out=w1_w_late[:].rearrange("p a c -> p (a c)").bitcast(FP8X4),
+            scales=w1_s_late[:].rearrange("p a c -> p (a c)"),
+            in_=w1_bf_late[:].rearrange("p a t m j -> p (a t m j)"),
+        )
+        for i in range(PACK, TILES):
             h_tile(i)
         damp_pair(0)
         damp_pair(2)
-        for i in range(4):
-            nc.scalar.activation(row(rest, i)[:, 0:256], root[i][:, 0:256], ACT.Copy, scale=gain_of(i))
+
+        apply_gain(0, 0, HALF)
         h_out(4)
         pick_ref(4)
-        make_z_pool(0)
-        make_z_pool(1)
-        for i in range(5, 8):
+        for b in range(2):
+            z_product(nc.gpsimd, z_first[:, b * P : (b + 1) * P], 0, b)
+        for i in range(5, TILES):
             h_out(i)
             pick_ref(i)
         damp_pair(4)
-        quantize_first()
-        open_block(0, 0, 4)
-        open_block(1, 0, 4)
+        z_w_first = held([P, HALF], U32, "h4")
+        for b in range(2):
+            z_codes[0, b] = z_w_first[:, b * P : (b + 1) * P]
+        nc.vector.quantize_mx(
+            out=z_w_first[:].bitcast(FP8X4),
+            scales=z_s[0][:, 0:HALF],
+            in_=z_first[:].rearrange("p j t -> p (j t)"),
+        )
+        for n0 in (0, 2):
+            y_passes(0, n0, n0 + 2, 0, 2)
         damp_pair(6)
-        for i in range(4, 8):
-            gain_s(i)
-        for i in range(4):
-            nc.scalar.activation(row(rest, i)[:, 256:NP], root[i][:, 256:NP], ACT.Copy, scale=gain_of(i))
+        apply_gain(1, 0, NP)
+        apply_gain(0, HALF, NP)
 
         make_z(1, 0)
         make_z(1, 1)
         quantize_z(1, 0)
-        close_block(0, 0, 4)
         make_z(0, 2)
         quantize_z(1, 1)
-        close_block(1, 0, 4)
+        for n0 in (0, 2):
+            y_passes(1, n0, n0 + 2, 0, 2)
         make_z(1, 2)
         quantize_z(0, 2)
-        open_block(2, 0, 4)
+        y_passes(0, 0, PACK, 2, 3)
         make_z(0, 3)
         quantize_z(1, 2)
-        close_block(2, 0, 4)
+        y_passes(1, 0, PACK, 2, 3)
         make_z(1, 3)
         quantize_z(0, 3)
-        open_block(3, 0, 2)
-        open_block(3, 2, 4)
+        for n0 in (0, 2):
+            y_passes(0, n0, n0 + 2, 3, 4)
         quantize_z(1, 3)
-        close_block(3, 0, 2)
-        close_block(3, 2, 4)
+        for n0 in (0, 2):
+            y_passes(1, n0, n0 + 2, 3, 4)

@@ -65,12 +65,18 @@ def tile_list_variant_pathogenicity_score_kernel(
         load_words(0)
         nc.sync.dma_start(offs_sb[:], offs)
         tab_s_words = tab_scales.bitcast(I32)
-        for q in range(4):
-            nc.sync.dma_start(tab_s[32 * q : 32 * q + 8, :], tab_s_words[:, 4 * q : 4 * q + 4, :])
-        nc.sync.dma_start(pos2_sb[:], pos2)
+
+        def load_scales(a):
+            for q in range(4):
+                rows = slice(32 * q + 4 * a, 32 * q + 4 * a + 4)
+                nc.sync.dma_start(tab_s[rows, :], tab_s_words[a, 4 * q : 4 * q + 4, :])
+
+        load_scales(0)
         load_w1(0, 0, 0, HALF)
+        load_scales(1)
         load_w1(0, 0, HALF, PASS)
         load_words(1)
+        nc.sync.dma_start(pos2_sb[:], pos2)
         load_w1(0, 1, 0, HALF)
         load_w1(0, 1, HALF, PASS)
         load_w1(1, 0, 0, HALF)
@@ -87,9 +93,10 @@ def tile_list_variant_pathogenicity_score_kernel(
             )
 
         v_s = held([P, S], U8, "v_s")
-        v_w = [held([P, S], U32, "v_w%d" % a) for a in range(2)]
+        v_w = {}
 
         def pick_words(a):
+            v_w[a] = held([P, S], U32, ("v_w0", "tab_s")[a])
             nc.vector.tensor_copy(v_w[a][:], tab_w[a][:].bitcast(U32).indirect(offs_sb[:]))
 
         w1_bf, w1_w, w1_s = {}, {}, {}

@@ -66,10 +66,11 @@ def tile_list_variant_pathogenicity_score_kernel(
         nc.sync.dma_start(offs_sb[:], offs)
         tab_s_words = tab_scales.bitcast(I32)
 
-        def load_scales(a):
-            for q in range(4):
-                rows = slice(32 * q + 4 * a, 32 * q + 4 * a + 4)
-                nc.sync.dma_start(tab_s[rows, :], tab_s_words[a, 4 * q : 4 * q + 4, :])
+        def load_scales(odd):
+            for q in (odd, odd + 2):
+                for a in range(2):
+                    rows = slice(32 * q + 4 * a, 32 * q + 4 * a + 4)
+                    nc.sync.dma_start(tab_s[rows, :], tab_s_words[a, 4 * q : 4 * q + 4, :])
 
         load_scales(0)
         load_w1(0, 0, 0, HALF)

@@ -23,6 +23,7 @@ PASS = P * PACK
 BANK = 512
 HALF = 256
 TILES = H // P
+EARLY = 3 * P
 
 
 def tile_list_variant_pathogenicity_score_kernel(
@@ -82,7 +83,8 @@ def tile_list_variant_pathogenicity_score_kernel(
         load_w1(0, 1, HALF, PASS)
         load_w1(1, 0, 0, HALF)
         load_w1(1, 0, HALF, PASS)
-        load_w1(1, 1, 0, PASS)
+        load_w1(1, 1, 0, HALF)
+        load_w1(1, 1, HALF, PASS)
         nc.sync.dma_start(pos1_sb[:], pos1)
         nc.sync.dma_start(gain_sb[:], gain.rearrange("(g p t) -> p g t", g=2, t=PACK))
         nc.sync.dma_start(w4_w[:].bitcast(I32), w4_words.rearrange("g p c -> p g c").bitcast(I32))
@@ -176,11 +178,7 @@ def tile_list_variant_pathogenicity_score_kernel(
             for n in (i, i + 1):
                 nc.scalar.activation(root[n][:], root[n][:], ACT.Abs_reciprocal_sqrt, bias=1.0)
             pick_var(i, 0, NP)
-            if i + 1 < TILES - 1:
-                pick_var(i + 1, 0, NP)
-            else:
-                pick_var(i + 1, 0, HALF)
-                pick_var(i + 1, HALF, NP)
+            pick_var(i + 1, 0, NP if i + 1 < TILES - 1 else HALF)
 
         def apply_gain(g, j0, j1):
             for t in range(PACK):
@@ -189,8 +187,8 @@ def tile_list_variant_pathogenicity_score_kernel(
 
         z_w = [held([P, NP], U32, "z_w%d" % g) for g in range(2)]
         z_s = [held([P, NP], U8, "z_s%d" % g) for g in range(2)]
-        z_first = held([P, HALF, PACK], BF16, "z_first")
-        z_codes = {(g, b): z_w[g][:, b * P : (b + 1) * P] for g in range(2) for b in range(4) if g == 1 or b >= 2}
+        z_first = held([P, EARLY, PACK], BF16, "z_first")
+        z_codes = {(g, b): z_w[g][:, b * P : (b + 1) * P] for g in range(2) for b in range(4) if g == 1 or b == 3}
         z_bf = {}
 
         def z_product(engine, dst, g, b):
@@ -218,18 +216,18 @@ def tile_list_variant_pathogenicity_score_kernel(
         out_v = out.rearrange("(nt p) j -> p nt j", p=P)
         y_bank = {}
 
-        def y_passes(g, n0, n1, b0, b1):
+        def y_passes(g, n0, n1, b0, b1, wide=1):
             if g == 0:
                 y_bank[n0, b0] = psum.tile([P, n1 - n0, (b1 - b0) * P], F32, name="bank")
             bank = y_bank[n0, b0]
-            for b in range(b0, b1):
+            for b in range(b0, b1, wide):
                 for nt in range(n0, n1):
                     nc.tensor.matmul_mx(
-                        out=bank[:, nt - n0, (b - b0) * P : (b - b0 + 1) * P],
+                        out=bank[:, nt - n0, (b - b0) * P : (b - b0 + wide) * P],
                         lhsT=w4_w[:, g, 2 * P * nt : 2 * P * (nt + 1)].bitcast(FP4X4),
                         lhsT_scale=w4_s8[:, g * N + P * nt : g * N + P * (nt + 1)],
                         rhs=z_codes[g, b].bitcast(FP8X4),
-                        rhs_scale=z_s[g][:, b * P : (b + 1) * P],
+                        rhs_scale=z_s[g][:, b * P : (b + wide) * P],
                         start=(g == 0 and (b, nt) == (b0, n0)),
                         stop=(g == 1 and (b, nt) == (b1 - 1, n1 - 1)),
                     )
@@ -264,15 +262,17 @@ def tile_list_variant_pathogenicity_score_kernel(
         w1_bf_late = held([P, 2, PACK, P, PACK], BF16, "w1_bf01")
         for a in range(2):
             w1_bf[1, a] = w1_bf_late[:, a]
-        round_w1(pool_round, 1, 0, 0)
+        round_w1(nc.vector.tensor_copy, 1, 0, 0, 0, 2)
+        round_w1(pool_round, 1, 0, 0, 2, PACK)
         h_out(0, (nc.scalar.copy, nc.vector.tensor_copy) * 2)
         round_w1(pool_round, 1, 0, HALF)
         pick_ref(0)
         for i in range(1, PACK):
             h_out(i)
             pick_ref(i)
-        round_w1(pool_round, 1, 1, 0, 2, PACK)
-        round_w1(nc.scalar.copy, 1, 1, 0, 0, 2)
+        round_w1(pool_round, 1, 1, 0)
+        round_w1(pool_round, 1, 1, HALF, 2, PACK)
+        round_w1(nc.scalar.copy, 1, 1, HALF, 0, 2)
         nc.vector.quantize_mx(
             out=w1_w_late[:].rearrange("p a c -> p (a c)").bitcast(FP8X4),
             scales=w1_s_late[:].rearrange("p a c -> p (a c)"),
@@ -283,38 +283,36 @@ def tile_list_variant_pathogenicity_score_kernel(
         damp_pair(0)
         damp_pair(2)
 
-        apply_gain(0, 0, HALF)
+        apply_gain(0, 0, EARLY)
         h_out(4)
         pick_ref(4)
-        for b in range(2):
+        for b in range(EARLY // P):
             z_product(nc.gpsimd, z_first[:, b * P : (b + 1) * P], 0, b)
         for i in range(5, TILES):
             h_out(i)
             pick_ref(i)
         damp_pair(4)
-        z_w_first = held([P, HALF], U32, "h4")
-        for b in range(2):
-            z_codes[0, b] = z_w_first[:, b * P : (b + 1) * P]
+        damp_pair(6)
+        z_w_first = held([P, EARLY], U32, "h6")
+        z_codes[0, 0], z_codes[0, 2] = z_w_first[:, 0:HALF], z_w_first[:, HALF:EARLY]
         nc.vector.quantize_mx(
             out=z_w_first[:].bitcast(FP8X4),
-            scales=z_s[0][:, 0:HALF],
+            scales=z_s[0][:, 0:EARLY],
             in_=z_first[:].rearrange("p j t -> p (j t)"),
         )
         for n0 in (0, 2):
-            y_passes(0, n0, n0 + 2, 0, 2)
-        damp_pair(6)
+            y_passes(0, n0, n0 + 2, 0, 2, 2)
+        pick_var(TILES - 1, HALF, NP)
         apply_gain(1, 0, NP)
-        apply_gain(0, HALF, NP)
+        apply_gain(0, EARLY, NP)
 
         make_z(1, 0)
         make_z(1, 1)
         quantize_z(1, 0)
-        make_z(0, 2)
+        make_z(1, 2)
         quantize_z(1, 1)
         for n0 in (0, 2):
             y_passes(1, n0, n0 + 2, 0, 2)
-        make_z(1, 2)
-        quantize_z(0, 2)
         y_passes(0, 0, PACK, 2, 3)
         make_z(0, 3)
         quantize_z(1, 2)

from contextlib import ExitStack

import concourse.mybir as mybir

K, T, S, NP, H, N = 1024, 2048, 1024, 512, 1024, 512
FLOPS = 2 * K * H * S + 2 * H * N * NP

F32 = mybir.dt.float32
BF16 = mybir.dt.bfloat16
I32 = mybir.dt.int32
U32 = mybir.dt.uint32
U16 = mybir.dt.uint16
U8 = mybir.dt.uint8
FP8X4 = mybir.dt.float8_e4m3fn_x4
FP4X4 = mybir.dt.float4_e2m1fn_x4
ACT = mybir.ActivationFunctionType
MULT = mybir.AluOpType.mult
ADD = mybir.AluOpType.add

P = 128
PACK = 4
PASS = P * PACK
BANK = 512
HALF = 256
TILES = H // P
EARLY = 3 * P


def tile_list_variant_pathogenicity_score_kernel(
    tc, tab_words, tab_scales, offs, pos1, pos2, w1, gain, w4_words, w4_scales, out
):
    nc = tc.nc
    with ExitStack() as ctx:
        keep = ctx.enter_context(tc.tile_pool(name="keep", bufs=1))
        psum = ctx.enter_context(tc.psum_pool(name="psum", bufs=8))

        def held(shape, dtype, name):
            return keep.tile(shape, dtype, name=name, align_bytes=64)

        offs_sb = keep.tile([P, S // 16], U16, name="offs_sb")
        pos1_sb = keep.tile([P, NP // 16], U16, name="pos1_sb")
        pos2_sb = keep.tile([P, NP // 16], U16, name="pos2_sb")
        tab_s = held([P, T // 4], I32, "tab_s")
        tab_w = [held([P, T], I32, "tab_w%d" % a) for a in range(2)]
        w4_s = held([P, 2 * N // 4], I32, "w4_s")
        w4_w = held([P, 2, 2 * N], U8, "w4_w")
        gain_sb = held([P, 2, PACK], F32, "gain_sb")

        nc.gpsimd.memset(tab_s[:], 0)
        one = held([P, 1], F32, "one")
        warm = held([P, 1], F32, "warm")
        nc.vector.memset(one[:], 1.0)
        nc.scalar.activation(warm[:], one[:], ACT.Abs_reciprocal_sqrt)
        nc.gpsimd.memset(w4_s[:], 0)

        w1_raw = {}

        def load_w1(g, a, c0, c1):
            w1_raw[g, a, c0] = held([P, PACK, c1 - c0], F32, "w1_raw%d%d_%d" % (g, a, c0))
            src = w1[a * PASS : (a + 1) * PASS, g * PASS + c0 : g * PASS + c1]
            nc.sync.dma_start(w1_raw[g, a, c0][:], src.rearrange("(p j) c -> p j c", j=PACK))

        def load_words(a):
            nc.sync.dma_start(tab_w[a][:], tab_words[a].rearrange("p t i -> p (t i)").bitcast(I32))

        load_words(0)
        nc.sync.dma_start(offs_sb[:], offs)
        tab_s_words = tab_scales.bitcast(I32)

        def load_scales(odd):
            for q in (odd, odd + 2):
                for a in range(2):
                    rows = slice(32 * q + 4 * a, 32 * q + 4 * a + 4)
                    nc.sync.dma_start(tab_s[rows, :], tab_s_words[a, 4 * q : 4 * q + 4, :])

        load_scales(0)
        load_w1(0, 0, 0, HALF)
        load_scales(1)
        load_w1(0, 0, HALF, PASS)
        load_words(1)
        nc.sync.dma_start(pos2_sb[:], pos2)
        load_w1(0, 1, 0, HALF)
        load_w1(0, 1, HALF, PASS)
        load_w1(1, 0, 0, HALF)
        load_w1(1, 0, HALF, PASS)
        load_w1(1, 1, 0, HALF)
        load_w1(1, 1, HALF, PASS)
        nc.sync.dma_start(pos1_sb[:], pos1)
        nc.sync.dma_start(gain_sb[:], gain.rearrange("(g p t) -> p g t", g=2, t=PACK))
        nc.sync.dma_start(w4_w[:].bitcast(I32), w4_words.rearrange("g p c -> p g c").bitcast(I32))
        w4_s_words = w4_scales.bitcast(I32)
        for q in range(4):
            nc.sync.dma_start(
                w4_s[32 * q : 32 * q + 4, :].rearrange("r (g c) -> r g c", g=2),
                w4_s_words[:, 4 * q : 4 * q + 4, :].rearrange("g r c -> r g c"),
            )

        v_s = held([P, S], U8, "v_s")
        v_w = {}

        def pick_words(a):
            v_w[a] = held([P, S], U32, ("v_w0", "tab_s")[a])
            nc.vector.tensor_copy(v_w[a][:], tab_w[a][:].bitcast(U32).indirect(offs_sb[:]))

        w1_bf, w1_w, w1_s = {}, {}, {}
        for a in range(2):
            w1_bf[0, a] = held([P, PACK, P, PACK], BF16, "w1_bf0%d" % a)[:]
            w1_w[0, a] = held([P, PASS], U32, "w1_w0%d" % a)[:]
            w1_s[0, a] = held([P, PASS], U8, "w1_s0%d" % a)[:]
        w1_w_late = held([P, 2, PASS], U32, "w1_w1")
        w1_s_late = held([P, 2, PASS], U8, "w1_s1")
        for a in range(2):
            w1_w[1, a] = w1_w_late[:, a]
            w1_s[1, a] = w1_s_late[:, a]

        def round_w1(copy, g, a, c0, t0=0, t1=PACK):
            src = w1_raw[g, a, c0][:].rearrange("p j (m t) -> p m j t", t=PACK)
            m0 = c0 // PACK
            dst = w1_bf[g, a].rearrange("p t m j -> p m j t")[:, m0 : m0 + src.shape[1]]
            copy(dst[:, :, :, t0:t1], src[:, :, :, t0:t1])

        def pool_round(dst, src):
            order = "p m j t -> p m t j"
            nc.gpsimd.tensor_scalar(dst.rearrange(order), src.rearrange(order), 1.0, 0.0, MULT, ADD)

        def quantize_w1(a, t0, t1):
            cols = slice(t0 * P, t1 * P)
            nc.vector.quantize_mx(
                out=w1_w[0, a][:, cols].bitcast(FP8X4),
                scales=w1_s[0, a][:, cols],
                in_=w1_bf[0, a][:, t0:t1].rearrange("p t m j -> p (t m j)"),
            )

        h = {}
        h_bank = {}

        def h_pass(i, a, u, width=BANK):
            g, t = divmod(i, PACK)
            cols = slice(t * P, (t + 1) * P)
            entries = slice(u * width, (u + 1) * width)
            if a == 0:
                h_bank[i, u] = psum.tile([P, width], F32, name="bank")
            nc.tensor.matmul_mx(
                out=h_bank[i, u][:],
                lhsT=w1_w[g, a][:, cols].bitcast(FP8X4),
                lhsT_scale=w1_s[g, a][:, cols],
                rhs=v_w[a][:, entries].bitcast(FP8X4),
                rhs_scale=v_s[4 * a : P, entries],
                start=(a == 0),
                stop=(a == 1),
            )

        def h_tile(i):
            for u in range(2):
                for a in range(2):
                    h_pass(i, a, u)

        def h_out(i, copies=(nc.scalar.copy, nc.scalar.copy)):
            h[i] = held([P, S], F32, "h%d" % i)
            width = S // len(copies)
            for u, copy in enumerate(copies):
                copy(h[i][:, u * width : (u + 1) * width], h_bank[i, u][:])

        root = [held([P, NP], F32, "root%d" % i) for i in range(TILES)]
        a_root = [held([P, PACK, NP], F32, "a_root%d" % g) for g in range(2)]
        gain_root = [held([P, PACK, NP], F32, "gain_root%d" % g) for g in range(2)]

        def pick_ref(i):
            nc.vector.tensor_copy(root[i][:], h[i][:].indirect(pos2_sb[:]))

        def pick_var(i, j0, j1):
            picked = h[i][:].indirect(pos1_sb[:, j0 // 16 : j1 // 16])
            nc.vector.tensor_tensor(a_root[i // PACK][:, i % PACK, j0:j1], picked, root[i][:, j0:j1], MULT)

        def damp_pair(i):
            for n in (i, i + 1):
                nc.scalar.activation(root[n][:], root[n][:], ACT.Square)
            for n in (i, i + 1):
                nc.scalar.activation(root[n][:], root[n][:], ACT.Abs_reciprocal_sqrt, bias=1.0)
            pick_var(i, 0, NP)
            pick_var(i + 1, 0, NP if i + 1 < TILES - 1 else HALF)

        def apply_gain(g, j0, j1):
            for t in range(PACK):
                scale = gain_sb[:, g, t : t + 1]
                nc.scalar.activation(gain_root[g][:, t, j0:j1], root[PACK * g + t][:, j0:j1], ACT.Copy, scale=scale)

        z_w = [held([P, NP], U32, "z_w%d" % g) for g in range(2)]
        z_s = [held([P, NP], U8, "z_s%d" % g) for g in range(2)]
        z_first = held([P, EARLY, PACK], BF16, "z_first")
        z_codes = {(g, b): z_w[g][:, b * P : (b + 1) * P] for g in range(2) for b in range(4) if g == 1 or b == 3}
        z_bf = {}

        def z_product(engine, dst, g, b):
            cols = slice(b * P, (b + 1) * P)
            engine.tensor_tensor(
                dst.rearrange("p (c e) t -> p c t e", e=4),
                a_root[g][:, :, cols].rearrange("p t (c e) -> p c t e", e=4),
                gain_root[g][:, :, cols].rearrange("p t (c e) -> p c t e", e=4),
                MULT,
            )

        def make_z(g, b):
            if b not in z_bf:
                z_bf[b] = keep.tile([P, 2, P, PACK], BF16, name="z_bf", align_bytes=64, bufs=2)
            z_product(nc.vector, z_bf[b][:, g], g, b)

        def quantize_z(g, b):
            nc.vector.quantize_mx(
                out=z_codes[g, b].bitcast(FP8X4),
                scales=z_s[g][:, b * P : (b + 1) * P],
                in_=z_bf[b][:, g].rearrange("p j t -> p (j t)"),
            )

        w4_s8 = w4_s[:].bitcast(U8)
        out_v = out.rearrange("(nt p) j -> p nt j", p=P)
        y_bank = {}

        def y_passes(g, n0, n1, b0, b1, wide=1):
            if g == 0:
                y_bank[n0, b0] = psum.tile([P, n1 - n0, (b1 - b0) * P], F32, name="bank")
            bank = y_bank[n0, b0]
            for b in range(b0, b1, wide):
                for nt in range(n0, n1):
                    nc.tensor.matmul_mx(
                        out=bank[:, nt - n0, (b - b0) * P : (b - b0 + wide) * P],
                        lhsT=w4_w[:, g, 2 * P * nt : 2 * P * (nt + 1)].bitcast(FP4X4),
                        lhsT_scale=w4_s8[:, g * N + P * nt : g * N + P * (nt + 1)],
                        rhs=z_codes[g, b].bitcast(FP8X4),
                        rhs_scale=z_s[g][:, b * P : (b + wide) * P],
                        start=(g == 0 and (b, nt) == (b0, n0)),
                        stop=(g == 1 and (b, nt) == (b1 - 1, n1 - 1)),
                    )
            if g == 1:
                res = held([P, n1 - n0, (b1 - b0) * P], F32, "res%d%d" % (n0, b0))
                nc.scalar.activation(res[:], bank[:], ACT.Sigmoid)
                nc.sync.dma_start(out_v[:, n0:n1, b0 * P : b1 * P], res[:])

        pick_words(0)
        nc.vector.tensor_copy(v_s[:], tab_s[:].bitcast(U8).indirect(offs_sb[:]))
        round_w1(nc.scalar.copy, 0, 0, 0)
        round_w1(nc.scalar.copy, 0, 0, HALF)
        first_tiles = ((0, 1), (1, 2), (2, PACK))
        for t0, t1 in first_tiles:
            quantize_w1(0, t0, t1)
        pick_words(1)
        round_w1(nc.scalar.copy, 0, 1, 0, 0, 2)
        round_w1(nc.scalar.copy, 0, 1, 0, 2, PACK)
        round_w1(nc.vector.tensor_copy, 0, 1, HALF, 0, 2)
        round_w1(nc.scalar.copy, 0, 1, HALF, 2, PACK)
        for t0, t1 in first_tiles:
            quantize_w1(1, t0, t1)
        for a in range(2):
            for u in range(4):
                h_pass(0, a, u, HALF)
        for i in (1, 2):
            for a in range(2):
                for u in range(2):
                    h_pass(i, a, u)
        h_tile(3)

        w1_bf_late = held([P, 2, PACK, P, PACK], BF16, "w1_bf01")
        for a in range(2):
            w1_bf[1, a] = w1_bf_late[:, a]
        round_w1(nc.vector.tensor_copy, 1, 0, 0, 0, 2)
        round_w1(pool_round, 1, 0, 0, 2, PACK)
        h_out(0, (nc.scalar.copy, nc.vector.tensor_copy) * 2)
        round_w1(pool_round, 1, 0, HALF)
        pick_ref(0)
        for i in range(1, PACK):
            h_out(i)
            pick_ref(i)
        round_w1(pool_round, 1, 1, 0)
        round_w1(pool_round, 1, 1, HALF, 2, PACK)
        round_w1(nc.scalar.copy, 1, 1, HALF, 0, 2)
        nc.vector.quantize_mx(
            out=w1_w_late[:].rearrange("p a c -> p (a c)").bitcast(FP8X4),
            scales=w1_s_late[:].rearrange("p a c -> p (a c)"),
            in_=w1_bf_late[:].rearrange("p a t m j -> p (a t m j)"),
        )
        for i in range(PACK, TILES):
            h_tile(i)
        damp_pair(0)
        damp_pair(2)

        apply_gain(0, 0, EARLY)
        h_out(4)
        pick_ref(4)
        for b in range(EARLY // P):
            z_product(nc.gpsimd, z_first[:, b * P : (b + 1) * P], 0, b)
        for i in range(5, TILES):
            h_out(i)
            pick_ref(i)
        damp_pair(4)
        damp_pair(6)
        z_w_first = held([P, EARLY], U32, "h6")
        z_codes[0, 0], z_codes[0, 2] = z_w_first[:, 0:HALF], z_w_first[:, HALF:EARLY]
        nc.vector.quantize_mx(
            out=z_w_first[:].bitcast(FP8X4),
            scales=z_s[0][:, 0:EARLY],
            in_=z_first[:].rearrange("p j t -> p (j t)"),
        )
        for n0 in (0, 2):
            y_passes(0, n0, n0 + 2, 0, 2, 2)
        pick_var(TILES - 1, HALF, NP)
        apply_gain(1, 0, NP)
        apply_gain(0, EARLY, NP)

        make_z(1, 0)
        make_z(1, 1)
        quantize_z(1, 0)
        make_z(1, 2)
        quantize_z(1, 1)
        for n0 in (0, 2):
            y_passes(1, n0, n0 + 2, 0, 2)
        y_passes(0, 0, PACK, 2, 3)
        make_z(0, 3)
        quantize_z(1, 2)
        y_passes(1, 0, PACK, 2, 3)
        make_z(1, 3)
        quantize_z(0, 3)
        for n0 in (0, 2):
            y_passes(0, n0, n0 + 2, 3, 4)
        quantize_z(1, 3)
        for n0 in (0, 2):
            y_passes(1, n0, n0 + 2, 3, 4)
